import numpy as np
import ml_dtypes


def mxq(x, axis, fmt="e4m3"):
    dtype, down = {"e4m3": (ml_dtypes.float8_e4m3fn, 7), "e5m2": (ml_dtypes.float8_e5m2, 14)}[fmt]
    v = np.moveaxis(np.asarray(x, np.float32).astype(ml_dtypes.bfloat16).astype(np.float64), axis, -1)
    blocks = v.reshape(v.shape[:-1] + (-1, 32))
    amax = np.abs(blocks).max(-1, keepdims=True)
    byte = np.maximum(np.where(amax > 0, np.frexp(amax)[1] - 1 + 127, 0) - down, 1)
    scale = np.exp2(byte - 127.0)
    codes = (blocks / scale).astype(np.float32).astype(dtype).astype(np.float64)
    return np.moveaxis((codes * scale).reshape(v.shape), -1, axis)


WIDE = False


def mx_kscale(k):
    if not WIDE:
        return np.ones(k)
    levels = np.array([10, -10, 5, -5, 0])
    if k % 512:
        return np.exp2(np.random.permutation(np.resize(levels, k // 32))).repeat(32)
    a = np.empty((k // 512, 16))
    for p in range(k // 512):
        a[p, :8] = np.random.permutation(np.resize(levels, 8))
        for g in range(8):
            far = levels[np.abs(levels - a[p, g]) >= 10]
            a[p, g + 8] = far[np.random.randint(len(far))]
    return np.exp2(a.ravel()).repeat(32)


def f64(x):
    return np.asarray(x).astype(np.float64)


def striped(idx):
    return np.tile(np.asarray(idx).reshape(-1, 16).T, (8, 1)).astype(np.uint16)


def unstriped(offs):
    return offs[:16].T.reshape(-1).astype(np.int64)


E2M1 = np.array([0.0, 0.5, 1.0, 1.5, 2.0, 3.0, 4.0, 6.0, -0.0, -0.5, -1.0, -1.5, -2.0, -3.0, -4.0, -6.0])


def pack_weight(w, fmt):
    k, n = w.shape
    w = f64(np.asarray(w, np.float32).astype(ml_dtypes.bfloat16)).reshape(k // 32, 32, n)
    amax = np.abs(w).max(1)
    if fmt == "e4m3":
        byte = np.frexp(amax)[1] - 1 + 127 - 7
    else:
        mant, ex = np.frexp(amax / 6.0)
        byte = np.where(mant > 0.5, ex, ex - 1) + 127
    byte = np.clip(np.where(amax > 0, byte, 1), 1, 254)
    scaled = (w * np.exp2(127.0 - byte)[:, None, :]).reshape(k, n).astype(np.float32)
    by_word = np.ascontiguousarray(scaled.reshape(k // 512, 128, 4, n).transpose(0, 1, 3, 2))
    if fmt == "e4m3":
        words = by_word.astype(ml_dtypes.float8_e4m3fn).view(np.uint8)
    else:
        c = by_word.astype(ml_dtypes.float4_e2m1fn).view(np.uint8) & 0xF
        words = (c[..., 0::2] | (c[..., 1::2] << 4)).reshape(k // 512, 128, 2 * n)
    return np.ascontiguousarray(words), np.ascontiguousarray(byte.astype(np.uint8).reshape(k // 512, 16, n))


def unpack_weight(words, scales, fmt):
    g, _, n = scales.shape
    words = np.ascontiguousarray(words).reshape(g, 128, n, -1)
    if fmt == "e4m3":
        vals = words.view(ml_dtypes.float8_e4m3fn).astype(np.float64)
    else:
        nib = np.empty((g, 128, n, 4), np.uint8)
        nib[..., 0::2] = words & 0xF
        nib[..., 1::2] = words >> 4
        vals = E2M1[nib]
    vals = vals * np.repeat(np.exp2(scales.astype(np.float64) - 127.0), 8, axis=1)[..., None]
    return vals.transpose(0, 1, 3, 2).reshape(g * 512, n)


B, N, T, D, NQ = 1, 512, 2048, 1024, 256


def setup_inputs():
    n = np.random.standard_normal
    idx = np.random.permutation(T)[:B * N]
    s = mx_kscale(D)[:, None]
    kp = pack_weight(n((D, T)) / s, "e2m1")
    return {
        "qT": (n((B, D, NQ)) * s * (1.00 / np.sqrt(D))).astype(np.float32),
        "k_words": np.ascontiguousarray(kp[0].reshape(1, 2, 128, T, 2).transpose(0, 2, 3, 1, 4)).reshape(1, 128, T, 4),
        "k_scales": kp[1],
        "ps": np.tile(np.random.randint(0, 64, 2048), (128, 1)).astype(np.float32),
        "sl": (np.random.uniform(0.01, 0.1, (B, NQ, 1))).astype(np.float32),
        "pq": (np.random.randint(0, 64, (B, NQ, 1))).astype(np.float32),
        "offs": striped(idx),
    }


def reference(qT, k_words, k_scales, ps, sl, pq, offs):
    idx = unstriped(offs)
    pick = lambda x, which: x[:, which].reshape(x.shape[0], B, -1).transpose(1, 0, 2)
    k = unpack_weight(k_words.reshape(1, 128, T, 2, 2).transpose(0, 3, 1, 2, 4).reshape(2, 128, 2 * T), k_scales, "e2m1")
    kg = pick(k, idx)
    qq = mxq(f64(qT), 1, "e4m3")
    a = qq.transpose(0, 2, 1) @ kg
    y = a - f64(sl) * np.abs(pick(f64(ps), idx)[:, :1, :] - f64(pq))
    return y

@@ -1,0 +1,128 @@
+from contextlib import ExitStack
+
+import concourse.mybir as mybir
+from concourse.masks import make_identity
+
+F32 = mybir.dt.float32
+BF16 = mybir.dt.bfloat16
+I32 = mybir.dt.int32
+U32 = mybir.dt.uint32
+U16 = mybir.dt.uint16
+U8 = mybir.dt.uint8
+FP8X4 = mybir.dt.float8_e4m3fn_x4
+FP4X4 = mybir.dt.float4_e2m1fn_x4
+ALU = mybir.AluOpType
+ACT = mybir.ActivationFunctionType
+
+P = 128
+N, T, D, NQ = 512, 2048, 1024, 256
+PASSES = D // 512
+TILES = NQ // P
+FLOPS = 2 * NQ * N * D
+
+
+def tile_attend_alibi_topk_kernel(tc, qT, k_words, k_scales, ps, sl, pq, offs, out):
+    nc = tc.nc
+    with ExitStack() as ctx:
+        sb = ctx.enter_context(tc.tile_pool(name="sb", bufs=1))
+        reuse = ctx.enter_context(tc.tile_pool(name="reuse", bufs=1))
+        psum = ctx.enter_context(tc.psum_pool(name="psum", bufs=1))
+        HALF = N // 2
+
+        offsets = sb.tile([P, N // 16], U16, name="offsets")
+        pos_win = reuse.tile([P, T], F32, name="pos_win", align_bytes=64, offset=0)
+        scale_win = reuse.tile([P, T], U8, name="scale_win", align_bytes=64, offset=4 * T)
+        word_win = sb.tile([P, T], U32, name="word_win", align_bytes=64)
+        plane1 = sb.tile([P, N], U8, name="plane1", align_bytes=64)
+        ident = sb.tile([P, P], F32, name="ident", align_bytes=64)
+
+        nc.vector.memset(pos_win[:], 0.0)
+        nc.gpsimd.memset(scale_win[:].bitcast(I32), 0)
+        nc.gpsimd.memset(plane1[:].bitcast(I32), 0)
+        make_identity(nc, ident[:])
+
+        raw = [reuse.tile([P, 4, NQ], F32, name="raw%d" % g, align_bytes=64, offset=6 * T + 16 * NQ * g) for g in range(PASSES)]
+        q_rows = qT[0].rearrange("(g p t) c -> g p t c", g=PASSES, t=4)
+
+        nc.sync.dma_start(offsets[:], offs)
+        nc.scalar.dma_start(raw[0][:], q_rows[0])
+        nc.scalar.dma_start(raw[1][:], q_rows[1])
+        nc.scalar.dma_start(word_win[:].bitcast(I32), k_words[0].rearrange("p t b -> p (t b)").bitcast(I32))
+        scale_rows = k_scales.bitcast(I32).rearrange("o (q j) n -> j q o n", j=4)
+        for j in range(4):
+            nc.sync.dma_start(scale_win[j:P:16, :].bitcast(I32), scale_rows[j])
+        nc.sync.dma_start(pos_win[0:1, :], ps[0:1, :])
+        slope = sb.tile([P, TILES], F32, name="slope")
+        qpos = sb.tile([P, TILES], F32, name="qpos")
+        with nc.allow_non_contiguous_dma(reason="one value a partition and query tile"):
+            nc.gpsimd.dma_start(qpos[:], pq[0].rearrange("(m p) o -> p (m o)", p=P))
+            nc.gpsimd.dma_start(slope[:], sl[0].rearrange("(m p) o -> p (m o)", p=P))
+        neg_slope = sb.tile([P, TILES], F32, name="neg_slope")
+        nc.gpsimd.tensor_scalar(neg_slope[:], slope[:], -1.0, 0.0, ALU.mult, ALU.add)
+
+        pos_g = sb.tile([P, N], F32, name="pos_g", align_bytes=64)
+        nc.vector.tensor_copy(pos_g[:], pos_win[:].indirect(offsets[:]))
+        scale_g = reuse.tile([P, N], U8, name="scale_g", align_bytes=64, offset=0)
+        nc.vector.tensor_copy(scale_g[:], scale_win[:].indirect(offsets[:]))
+        nc.sync.dma_start(plane1[0:P - 16, :].bitcast(I32), scale_g[16:P, :].bitcast(I32))
+        key_planes = [scale_g, plane1]
+
+        q_planes = reuse.tile([P, PASSES, NQ], U8, name="q_planes", align_bytes=64, offset=4 * T)
+        codes = []
+        for g in range(PASSES):
+            grouped = sb.tile([P, NQ, 4], BF16, name="grouped%d" % g, align_bytes=64)
+            codes.append(sb.tile([P, NQ], U32, name="codes%d" % g, align_bytes=64))
+            for m in range(TILES):
+                cols = slice(m * P, (m + 1) * P)
+                nc.scalar.copy(
+                    grouped[:, cols, :].rearrange("p (c i) t -> p c t i", i=4),
+                    raw[g][:, :, cols].rearrange("p t (c i) -> p c t i", i=4),
+                )
+            nc.vector.quantize_mx(
+                out=codes[g][:].bitcast(FP8X4),
+                scales=q_planes[:, g, :],
+                in_=grouped[:].rearrange("p c t -> p (c t)"),
+            )
+
+        turned = psum.tile([P, 4, P], F32, name="turned")
+        for c in range(4):
+            nc.tensor.transpose(turned[:, c, :], pos_g[:, c * P:(c + 1) * P], ident[:])
+        pos_col = reuse.tile([P, 4], F32, name="pos_col", align_bytes=64, offset=6 * T + 16 * NQ * PASSES - 64)
+        nc.scalar.copy(pos_col[:], turned[:, :, 0])
+        spread = psum.tile([P, N], F32, name="spread")
+        for c in range(4):
+            nc.tensor.transpose(spread[:, c * P:(c + 1) * P], pos_col[:, c:c + 1].to_broadcast([P, P]), ident[:])
+        dist = []
+        for m in range(TILES):
+            dist.append(sb.tile([P, N], F32, name="dist%d" % m, align_bytes=64))
+            nc.scalar.activation(dist[m][:], spread[:], ACT.Abs, bias=qpos[:, m:m + 1], scale=-1.0)
+
+        keys = []
+        for h in range(2):
+            word_g = reuse.tile([P, HALF], U32, name="word_g%d" % h, align_bytes=64,
+                                offset=4 * T + PASSES * NQ + 4 * HALF * h)
+            nc.vector.tensor_copy(word_g[:], word_win[:].indirect(offsets[:, h * HALF // 16:(h + 1) * HALF // 16]))
+            keys.append(sb.tile([P, PASSES, HALF], U16, name="keys%d" % h, align_bytes=64))
+            nc.vector.tensor_copy(keys[h][:], word_g[:].bitcast(U16).rearrange("p (n g) -> p g n", g=PASSES))
+
+        for h in range(2):
+            slots = slice(h * HALF, (h + 1) * HALF)
+            for m in range(TILES):
+                cols = slice(m * P, (m + 1) * P)
+                acc = psum.tile([P, HALF], F32, name="acc%d%d" % (h, m))
+                for b in range(HALF // P):
+                    for g in range(PASSES):
+                        nc.tensor.matmul_mx(
+                            out=acc[:, b * P:(b + 1) * P],
+                            lhsT=codes[g][:, cols].bitcast(FP8X4),
+                            lhsT_scale=q_planes[:, g, cols],
+                            rhs=keys[h][:, g, b * P:(b + 1) * P].bitcast(FP4X4),
+                            rhs_scale=key_planes[g][:, h * HALF + b * P:h * HALF + (b + 1) * P],
+                            start=(g == 0),
+                            stop=(g == PASSES - 1),
+                        )
+                result = sb.tile([P, HALF], F32, name="result%d%d" % (h, m), align_bytes=64)
+                nc.vector.scalar_tensor_tensor(
+                    result[:], dist[m][:, slots], neg_slope[:, m:m + 1], acc[:], ALU.mult, ALU.add
+                )
+                nc.sync.dma_start(out[0, cols, slots], result[:])

@@ -25,104 +25,122 @@ def tile_attend_alibi_topk_kernel(tc, qT, k_words, k_scales, ps, sl, pq, offs, o
     nc = tc.nc
     with ExitStack() as ctx:
         sb = ctx.enter_context(tc.tile_pool(name="sb", bufs=1))
-        reuse = ctx.enter_context(tc.tile_pool(name="reuse", bufs=1))
         psum = ctx.enter_context(tc.psum_pool(name="psum", bufs=1))
-        HALF = N // 2
+        QUARTER = 96
 
         offsets = sb.tile([P, N // 16], U16, name="offsets")
-        pos_win = reuse.tile([P, T], F32, name="pos_win", align_bytes=64, offset=0)
-        scale_win = reuse.tile([P, T], U8, name="scale_win", align_bytes=64, offset=4 * T)
-        word_win = sb.tile([P, T], U32, name="word_win", align_bytes=64)
+        pos_win = sb.tile([P, T], F32, name="pos_win", align_bytes=64)
+        scale_win = sb.tile([P, T], U8, name="scale_win", align_bytes=64)
         plane1 = sb.tile([P, N], U8, name="plane1", align_bytes=64)
         ident = sb.tile([P, P], F32, name="ident", align_bytes=64)
 
-        nc.vector.memset(pos_win[:], 0.0)
-        nc.gpsimd.memset(scale_win[:].bitcast(I32), 0)
-        nc.gpsimd.memset(plane1[:].bitcast(I32), 0)
+        nc.vector.memset(scale_win[:].bitcast(I32), 0)
+        nc.vector.memset(pos_win[0:QUARTER, :], 0.0)
         make_identity(nc, ident[:])
+        nc.gpsimd.memset(plane1[:].bitcast(I32), 0)
 
-        raw = [reuse.tile([P, 4, NQ], F32, name="raw%d" % g, align_bytes=64, offset=6 * T + 16 * NQ * g) for g in range(PASSES)]
-        q_rows = qT[0].rearrange("(g p t) c -> g p t c", g=PASSES, t=4)
+        word_win = sb.tile([P, T], U32, name="word_win", align_bytes=64)
+        raw = sb.tile([P, PASSES * 4 * NQ], F32, name="raw", align_bytes=64)
+        q_rows = qT[0].rearrange("(g p t) c -> g p (t c)", g=PASSES, t=4)
 
         nc.sync.dma_start(offsets[:], offs)
-        nc.scalar.dma_start(raw[0][:], q_rows[0])
-        nc.scalar.dma_start(raw[1][:], q_rows[1])
-        nc.scalar.dma_start(word_win[:].bitcast(I32), k_words[0].rearrange("p t b -> p (t b)").bitcast(I32))
+        nc.sync.dma_start(pos_win[QUARTER:P, :], ps[QUARTER:P, :])
         scale_rows = k_scales.bitcast(I32).rearrange("o (q j) n -> j q o n", j=4)
+        words = k_words[0].rearrange("p t b -> p (t b)").bitcast(I32)
+        nc.sync.dma_start(word_win[:, 0:T // 2].bitcast(I32), words[:, 0:T // 2])
         for j in range(4):
             nc.sync.dma_start(scale_win[j:P:16, :].bitcast(I32), scale_rows[j])
-        nc.sync.dma_start(pos_win[0:1, :], ps[0:1, :])
-        slope = sb.tile([P, TILES], F32, name="slope")
-        qpos = sb.tile([P, TILES], F32, name="qpos")
+        nc.sync.dma_start(word_win[:, T // 2:T].bitcast(I32), words[:, T // 2:T])
+        for g in range(PASSES):
+            nc.sync.dma_start(raw[:, g * 4 * NQ:(g + 1) * 4 * NQ], q_rows[g])
+        slope = sb.tile([P, TILES], F32, name="slope", align_bytes=64)
+        qpos = sb.tile([P, TILES], F32, name="qpos", align_bytes=64)
         with nc.allow_non_contiguous_dma(reason="one value a partition and query tile"):
-            nc.gpsimd.dma_start(qpos[:], pq[0].rearrange("(m p) o -> p (m o)", p=P))
-            nc.gpsimd.dma_start(slope[:], sl[0].rearrange("(m p) o -> p (m o)", p=P))
+            nc.sync.dma_start(qpos[:], pq[0].rearrange("(m p) o -> p (m o)", p=P))
+            nc.sync.dma_start(slope[:], sl[0].rearrange("(m p) o -> p (m o)", p=P))
         neg_slope = sb.tile([P, TILES], F32, name="neg_slope")
         nc.gpsimd.tensor_scalar(neg_slope[:], slope[:], -1.0, 0.0, ALU.mult, ALU.add)
 
         pos_g = sb.tile([P, N], F32, name="pos_g", align_bytes=64)
         nc.vector.tensor_copy(pos_g[:], pos_win[:].indirect(offsets[:]))
-        scale_g = reuse.tile([P, N], U8, name="scale_g", align_bytes=64, offset=0)
+        scale_g = sb.tile([P, N], U8, name="scale_g", align_bytes=64)
         nc.vector.tensor_copy(scale_g[:], scale_win[:].indirect(offsets[:]))
-        nc.sync.dma_start(plane1[0:P - 16, :].bitcast(I32), scale_g[16:P, :].bitcast(I32))
-        key_planes = [scale_g, plane1]
-
-        q_planes = reuse.tile([P, PASSES, NQ], U8, name="q_planes", align_bytes=64, offset=4 * T)
-        codes = []
-        for g in range(PASSES):
-            grouped = sb.tile([P, NQ, 4], BF16, name="grouped%d" % g, align_bytes=64)
-            codes.append(sb.tile([P, NQ], U32, name="codes%d" % g, align_bytes=64))
-            for m in range(TILES):
-                cols = slice(m * P, (m + 1) * P)
-                nc.scalar.copy(
-                    grouped[:, cols, :].rearrange("p (c i) t -> p c t i", i=4),
-                    raw[g][:, :, cols].rearrange("p t (c i) -> p c t i", i=4),
-                )
-            nc.vector.quantize_mx(
-                out=codes[g][:].bitcast(FP8X4),
-                scales=q_planes[:, g, :],
-                in_=grouped[:].rearrange("p c t -> p (c t)"),
+        for first, count in ((32, 64), (0, 4), (96, 4)):
+            nc.sync.dma_start(
+                plane1[first:first + count, :].bitcast(I32), scale_g[first + 16:first + 16 + count, :].bitcast(I32)
             )
+        key_planes = [scale_g, plane1]
 
         turned = psum.tile([P, 4, P], F32, name="turned")
         for c in range(4):
             nc.tensor.transpose(turned[:, c, :], pos_g[:, c * P:(c + 1) * P], ident[:])
-        pos_col = reuse.tile([P, 4], F32, name="pos_col", align_bytes=64, offset=6 * T + 16 * NQ * PASSES - 64)
-        nc.scalar.copy(pos_col[:], turned[:, :, 0])
+        pos_col = sb.tile([P, 4], F32, name="pos_col")
+        nc.scalar.copy(pos_col[:], turned[:, :, QUARTER])
         spread = psum.tile([P, N], F32, name="spread")
         for c in range(4):
             nc.tensor.transpose(spread[:, c * P:(c + 1) * P], pos_col[:, c:c + 1].to_broadcast([P, P]), ident[:])
+
+        word_g = sb.tile([P, N], U32, name="word_g", align_bytes=64)
+        nc.vector.tensor_copy(word_g[:], word_win[:].indirect(offsets[:]))
+        halves = word_g[:].bitcast(U16).rearrange("p (n g) -> p g n", g=PASSES)
+        keys = []
+        for g in range(PASSES):
+            keys.append(sb.tile([P, N], U16, name="keys%d" % g, align_bytes=64))
+
+        codes = {}
+        planes = {}
+        grouped = {}
+
+        def cast(copy, g, m):
+            grouped[g, m] = sb.tile([P, P, 4], BF16, name="grouped%d%d" % (g, m), align_bytes=64)
+            rows = raw[:, g * 4 * NQ:(g + 1) * 4 * NQ].rearrange("p (t c) -> p t c", t=4)
+            copy(
+                grouped[g, m][:].rearrange("p (c i) t -> p c t i", i=4),
+                rows[:, :, m * P:(m + 1) * P].rearrange("p t (c i) -> p c t i", i=4),
+            )
+
+        def quantise(g, m):
+            codes[g, m] = sb.tile([P, P], U32, name="codes%d%d" % (g, m), align_bytes=64)
+            planes[g, m] = sb.tile([P, P], U8, name="plane%d%d" % (g, m), align_bytes=64)
+            nc.vector.quantize_mx(
+                out=codes[g, m][:].bitcast(FP8X4),
+                scales=planes[g, m][:],
+                in_=grouped[g, m][:].rearrange("p c t -> p (c t)"),
+            )
+
+        cast(nc.scalar.copy, 0, 0)
+        cast(nc.scalar.copy, 0, 1)
+        cast(nc.scalar.copy, 1, 0)
+        nc.vector.tensor_copy(keys[0][:], halves[:, 0, :])
+        quantise(0, 0)
+        nc.vector.tensor_copy(keys[1][:], halves[:, 1, :])
+        cast(nc.vector.tensor_copy, 1, 1)
+        quantise(1, 0)
+        quantise(0, 1)
+        quantise(1, 1)
+
         dist = []
         for m in range(TILES):
             dist.append(sb.tile([P, N], F32, name="dist%d" % m, align_bytes=64))
             nc.scalar.activation(dist[m][:], spread[:], ACT.Abs, bias=qpos[:, m:m + 1], scale=-1.0)
 
-        keys = []
-        for h in range(2):
-            word_g = reuse.tile([P, HALF], U32, name="word_g%d" % h, align_bytes=64,
-                                offset=4 * T + PASSES * NQ + 4 * HALF * h)
-            nc.vector.tensor_copy(word_g[:], word_win[:].indirect(offsets[:, h * HALF // 16:(h + 1) * HALF // 16]))
-            keys.append(sb.tile([P, PASSES, HALF], U16, name="keys%d" % h, align_bytes=64))
-            nc.vector.tensor_copy(keys[h][:], word_g[:].bitcast(U16).rearrange("p (n g) -> p g n", g=PASSES))
-
-        for h in range(2):
-            slots = slice(h * HALF, (h + 1) * HALF)
-            for m in range(TILES):
-                cols = slice(m * P, (m + 1) * P)
-                acc = psum.tile([P, HALF], F32, name="acc%d%d" % (h, m))
-                for b in range(HALF // P):
-                    for g in range(PASSES):
-                        nc.tensor.matmul_mx(
-                            out=acc[:, b * P:(b + 1) * P],
-                            lhsT=codes[g][:, cols].bitcast(FP8X4),
-                            lhsT_scale=q_planes[:, g, cols],
-                            rhs=keys[h][:, g, b * P:(b + 1) * P].bitcast(FP4X4),
-                            rhs_scale=key_planes[g][:, h * HALF + b * P:h * HALF + (b + 1) * P],
-                            start=(g == 0),
-                            stop=(g == PASSES - 1),
-                        )
-                result = sb.tile([P, HALF], F32, name="result%d%d" % (h, m), align_bytes=64)
-                nc.vector.scalar_tensor_tensor(
-                    result[:], dist[m][:, slots], neg_slope[:, m:m + 1], acc[:], ALU.mult, ALU.add
-                )
-                nc.sync.dma_start(out[0, cols, slots], result[:])
+        for m, first, count, width in ((0, 0, N, N), (1, 0, N // 2, P), (1, N // 2, N // 2, P)):
+            acc = psum.tile([P, count], F32, name="acc%d%d" % (m, first))
+            for n0 in range(0, count, width):
+                slots = slice(first + n0, first + n0 + width)
+                for g in range(PASSES):
+                    nc.tensor.matmul_mx(
+                        out=acc[:, n0:n0 + width],
+                        lhsT=codes[g, m][:].bitcast(FP8X4),
+                        lhsT_scale=planes[g, m][:],
+                        rhs=keys[g][:, slots].bitcast(FP4X4),
+                        rhs_scale=key_planes[g][:, slots],
+                        start=(g == 0),
+                        stop=(g == PASSES - 1),
+                    )
+            slots = slice(first, first + count)
+            result = sb.tile([P, count], F32, name="result%d%d" % (m, first), align_bytes=64)
+            nc.vector.scalar_tensor_tensor(
+                result[:], dist[m][:, slots], neg_slope[:, m:m + 1], acc[:], ALU.mult, ALU.add
+            )
+            nc.sync.dma_start(out[0, m * P:(m + 1) * P, slots], result[:])

@@ -47,10 +47,10 @@ def tile_attend_alibi_topk_kernel(tc, qT, k_words, k_scales, ps, sl, pq, offs, o
         nc.sync.dma_start(pos_win[QUARTER:P, :], ps[QUARTER:P, :])
         scale_rows = k_scales.bitcast(I32).rearrange("o (q j) n -> j q o n", j=4)
         words = k_words[0].rearrange("p t b -> p (t b)").bitcast(I32)
-        nc.sync.dma_start(word_win[:, 0:T // 2].bitcast(I32), words[:, 0:T // 2])
+        nc.sync.dma_start(word_win[:, 0:T // 4].bitcast(I32), words[:, 0:T // 4])
         for j in range(4):
             nc.sync.dma_start(scale_win[j:P:16, :].bitcast(I32), scale_rows[j])
-        nc.sync.dma_start(word_win[:, T // 2:T].bitcast(I32), words[:, T // 2:T])
+        nc.sync.dma_start(word_win[:, T // 4:T].bitcast(I32), words[:, T // 4:T])
         for g in range(PASSES):
             nc.sync.dma_start(raw[:, g * 4 * NQ:(g + 1) * 4 * NQ], q_rows[g])
         slope = sb.tile([P, TILES], F32, name="slope", align_bytes=64)
@@ -111,12 +111,12 @@ def tile_attend_alibi_topk_kernel(tc, qT, k_words, k_scales, ps, sl, pq, offs, o
         cast(nc.scalar.copy, 0, 0)
         cast(nc.scalar.copy, 0, 1)
         cast(nc.scalar.copy, 1, 0)
+        cast(nc.scalar.copy, 1, 1)
         nc.vector.tensor_copy(keys[0][:], halves[:, 0, :])
         quantise(0, 0)
         nc.vector.tensor_copy(keys[1][:], halves[:, 1, :])
-        cast(nc.vector.tensor_copy, 1, 1)
-        quantise(1, 0)
         quantise(0, 1)
+        quantise(1, 0)
         quantise(1, 1)
 
         dist = []
@@ -124,7 +124,9 @@ def tile_attend_alibi_topk_kernel(tc, qT, k_words, k_scales, ps, sl, pq, offs, o
             dist.append(sb.tile([P, N], F32, name="dist%d" % m, align_bytes=64))
             nc.scalar.activation(dist[m][:], spread[:], ACT.Abs, bias=qpos[:, m:m + 1], scale=-1.0)
 
-        for m, first, count, width in ((0, 0, N, N), (1, 0, N // 2, P), (1, N // 2, N // 2, P)):
+        for m, first, count, width, queue in (
+            (0, 0, N, N, nc.sync), (1, 0, N // 2, P, nc.sync), (1, N // 2, N // 2, P, nc.scalar)
+        ):
             acc = psum.tile([P, count], F32, name="acc%d%d" % (m, first))
             for n0 in range(0, count, width):
                 slots = slice(first + n0, first + n0 + width)
@@ -143,4 +145,4 @@ def tile_attend_alibi_topk_kernel(tc, qT, k_words, k_scales, ps, sl, pq, offs, o
             nc.vector.scalar_tensor_tensor(
                 result[:], dist[m][:, slots], neg_slope[:, m:m + 1], acc[:], ALU.mult, ALU.add
             )
-            nc.sync.dma_start(out[0, m * P:(m + 1) * P, slots], result[:])
+            queue.dma_start(out[0, m * P:(m + 1) * P, slots], result[:])

@@ -124,9 +124,7 @@ def tile_attend_alibi_topk_kernel(tc, qT, k_words, k_scales, ps, sl, pq, offs, o
             dist.append(sb.tile([P, N], F32, name="dist%d" % m, align_bytes=64))
             nc.scalar.activation(dist[m][:], spread[:], ACT.Abs, bias=qpos[:, m:m + 1], scale=-1.0)
 
-        for m, first, count, width, queue in (
-            (0, 0, N, N, nc.sync), (1, 0, N // 2, P, nc.sync), (1, N // 2, N // 2, P, nc.scalar)
-        ):
+        for m, first, count, width in ((0, 0, N, N), (1, 0, N // 2, P), (1, N // 2, N // 2, P)):
             acc = psum.tile([P, count], F32, name="acc%d%d" % (m, first))
             for n0 in range(0, count, width):
                 slots = slice(first + n0, first + n0 + width)
@@ -145,4 +143,4 @@ def tile_attend_alibi_topk_kernel(tc, qT, k_words, k_scales, ps, sl, pq, offs, o
             nc.vector.scalar_tensor_tensor(
                 result[:], dist[m][:, slots], neg_slope[:, m:m + 1], acc[:], ALU.mult, ALU.add
             )
-            queue.dma_start(out[0, m * P:(m + 1) * P, slots], result[:])
+            nc.sync.dma_start(out[0, m * P:(m + 1) * P, slots], result[:])

@@ -26,77 +26,48 @@ def tile_attend_alibi_topk_kernel(tc, qT, k_words, k_scales, ps, sl, pq, offs, o
     with ExitStack() as ctx:
         sb = ctx.enter_context(tc.tile_pool(name="sb", bufs=1))
         psum = ctx.enter_context(tc.psum_pool(name="psum", bufs=1))
-        QUARTER = 96
+        LAST = P - 1
+        ROWS = P - 2 * TILES
+        HALF = N // 2
 
         offsets = sb.tile([P, N // 16], U16, name="offsets")
         pos_win = sb.tile([P, T], F32, name="pos_win", align_bytes=64)
         scale_win = sb.tile([P, T], U8, name="scale_win", align_bytes=64)
+        word_win = sb.tile([P, T], U32, name="word_win", align_bytes=64)
         plane1 = sb.tile([P, N], U8, name="plane1", align_bytes=64)
         ident = sb.tile([P, P], F32, name="ident", align_bytes=64)
+        row_consts = sb.tile([P, P], F32, name="row_consts", align_bytes=64)
+        raw = [sb.tile([P, 4, NQ], F32, name="raw%d" % g, align_bytes=64) for g in range(PASSES)]
 
         nc.vector.memset(scale_win[:].bitcast(I32), 0)
-        nc.vector.memset(pos_win[0:QUARTER, :], 0.0)
+        nc.vector.memset(pos_win[0:LAST, :], 0.0)
         make_identity(nc, ident[:])
         nc.gpsimd.memset(plane1[:].bitcast(I32), 0)
+        nc.gpsimd.memset(row_consts[0:ROWS, :], 0.0)
 
-        word_win = sb.tile([P, T], U32, name="word_win", align_bytes=64)
-        raw = sb.tile([P, PASSES * 4 * NQ], F32, name="raw", align_bytes=64)
-        q_rows = qT[0].rearrange("(g p t) c -> g p (t c)", g=PASSES, t=4)
-
-        nc.sync.dma_start(offsets[:], offs)
-        nc.sync.dma_start(pos_win[QUARTER:P, :], ps[QUARTER:P, :])
+        q_rows = qT[0].rearrange("(g p t) c -> g p t c", g=PASSES, t=4)
         scale_rows = k_scales.bitcast(I32).rearrange("o (q j) n -> j q o n", j=4)
         words = k_words[0].rearrange("p t b -> p (t b)").bitcast(I32)
-        nc.sync.dma_start(word_win[:, 0:T // 4].bitcast(I32), words[:, 0:T // 4])
+
+        nc.sync.dma_start(offsets[:], offs)
+        nc.sync.dma_start(pos_win[LAST:P, :], ps[0:1, :])
+        nc.sync.dma_start(raw[0][:], q_rows[0])
         for j in range(4):
             nc.sync.dma_start(scale_win[j:P:16, :].bitcast(I32), scale_rows[j])
-        nc.sync.dma_start(word_win[:, T // 4:T].bitcast(I32), words[:, T // 4:T])
-        for g in range(PASSES):
-            nc.sync.dma_start(raw[:, g * 4 * NQ:(g + 1) * 4 * NQ], q_rows[g])
-        slope = sb.tile([P, TILES], F32, name="slope", align_bytes=64)
-        qpos = sb.tile([P, TILES], F32, name="qpos", align_bytes=64)
-        with nc.allow_non_contiguous_dma(reason="one value a partition and query tile"):
-            nc.sync.dma_start(qpos[:], pq[0].rearrange("(m p) o -> p (m o)", p=P))
-            nc.sync.dma_start(slope[:], sl[0].rearrange("(m p) o -> p (m o)", p=P))
-        neg_slope = sb.tile([P, TILES], F32, name="neg_slope")
-        nc.gpsimd.tensor_scalar(neg_slope[:], slope[:], -1.0, 0.0, ALU.mult, ALU.add)
-
-        pos_g = sb.tile([P, N], F32, name="pos_g", align_bytes=64)
-        nc.vector.tensor_copy(pos_g[:], pos_win[:].indirect(offsets[:]))
-        scale_g = sb.tile([P, N], U8, name="scale_g", align_bytes=64)
-        nc.vector.tensor_copy(scale_g[:], scale_win[:].indirect(offsets[:]))
-        for first, count in ((32, 64), (0, 4), (96, 4)):
-            nc.sync.dma_start(
-                plane1[first:first + count, :].bitcast(I32), scale_g[first + 16:first + 16 + count, :].bitcast(I32)
-            )
-        key_planes = [scale_g, plane1]
-
-        turned = psum.tile([P, 4, P], F32, name="turned")
-        for c in range(4):
-            nc.tensor.transpose(turned[:, c, :], pos_g[:, c * P:(c + 1) * P], ident[:])
-        pos_col = sb.tile([P, 4], F32, name="pos_col")
-        nc.scalar.copy(pos_col[:], turned[:, :, QUARTER])
-        spread = psum.tile([P, N], F32, name="spread")
-        for c in range(4):
-            nc.tensor.transpose(spread[:, c * P:(c + 1) * P], pos_col[:, c:c + 1].to_broadcast([P, P]), ident[:])
-
-        word_g = sb.tile([P, N], U32, name="word_g", align_bytes=64)
-        nc.vector.tensor_copy(word_g[:], word_win[:].indirect(offsets[:]))
-        halves = word_g[:].bitcast(U16).rearrange("p (n g) -> p g n", g=PASSES)
-        keys = []
-        for g in range(PASSES):
-            keys.append(sb.tile([P, N], U16, name="keys%d" % g, align_bytes=64))
+        nc.sync.dma_start(row_consts[ROWS:ROWS + TILES, :], pq[0].rearrange("(m p) o -> m (p o)", p=P))
+        nc.sync.dma_start(row_consts[ROWS + TILES:P, :], sl[0].rearrange("(m p) o -> m (p o)", p=P))
+        nc.sync.dma_start(word_win[:].bitcast(I32), words)
+        nc.sync.dma_start(raw[1][:], q_rows[1])
 
         codes = {}
         planes = {}
         grouped = {}
 
-        def cast(copy, g, m):
-            grouped[g, m] = sb.tile([P, P, 4], BF16, name="grouped%d%d" % (g, m), align_bytes=64)
-            rows = raw[:, g * 4 * NQ:(g + 1) * 4 * NQ].rearrange("p (t c) -> p t c", t=4)
+        def cast(copy, g, m, tag):
+            grouped[g, m] = sb.tile([P, P, 4], BF16, name="grouped%d%d" % (g, m), tag=tag, align_bytes=64)
             copy(
                 grouped[g, m][:].rearrange("p (c i) t -> p c t i", i=4),
-                rows[:, :, m * P:(m + 1) * P].rearrange("p t (c i) -> p c t i", i=4),
+                raw[g][:, :, m * P:(m + 1) * P].rearrange("p t (c i) -> p c t i", i=4),
             )
 
         def quantise(g, m):
@@ -108,39 +79,87 @@ def tile_attend_alibi_topk_kernel(tc, qT, k_words, k_scales, ps, sl, pq, offs, o
                 in_=grouped[g, m][:].rearrange("p c t -> p (c t)"),
             )
 
-        cast(nc.scalar.copy, 0, 0)
-        cast(nc.scalar.copy, 0, 1)
-        cast(nc.scalar.copy, 1, 0)
-        cast(nc.scalar.copy, 1, 1)
-        nc.vector.tensor_copy(keys[0][:], halves[:, 0, :])
+        pos_g = sb.tile([P, N], F32, name="pos_g", align_bytes=64)
+        nc.vector.tensor_copy(pos_g[:], pos_win[:].indirect(offsets[:]))
+        turned = psum.tile([P, 4, P], F32, name="turned", tag="turned")
+        for c in range(4):
+            nc.tensor.transpose(turned[:, c, :], pos_g[:, c * P:(c + 1) * P], ident[:])
+        cast(nc.scalar.copy, 0, 0, "grouped00")
+        pos_col = sb.tile([P, 4], F32, name="pos_col")
+        nc.scalar.copy(pos_col[:], turned[:, :, LAST])
+        cast(nc.scalar.copy, 0, 1, "grouped01")
+        consts_t = psum.tile([P, P], F32, name="consts_t", tag="late1")
+        nc.tensor.transpose(consts_t[:], row_consts[:], ident[:])
+        consts = sb.tile([P, 2 * TILES], F32, name="consts")
+        nc.scalar.copy(consts[:], consts_t[:, ROWS:P])
+        spread = psum.tile([P, N], F32, name="spread")
+        for c in range(4):
+            nc.tensor.transpose(spread[:, c * P:(c + 1) * P], pos_col[:, c:c + 1].to_broadcast([P, P]), ident[:])
+        dist = [sb.tile([P, N], F32, name="dist%d" % m, align_bytes=64) for m in range(TILES)]
+        for m in range(TILES):
+            nc.scalar.activation(dist[m][:], spread[:], ACT.Abs, bias=consts[:, m:m + 1], scale=-1.0)
+
+        scale_g = sb.tile([P, N], U8, name="scale_g", align_bytes=64)
+        nc.vector.tensor_copy(scale_g[:], scale_win[:].indirect(offsets[:]))
+        for first, count in ((32, 64), (0, 4), (96, 4)):
+            nc.sync.dma_start(
+                plane1[first:first + count, :].bitcast(I32), scale_g[first + 16:first + 16 + count, :].bitcast(I32)
+            )
+        key_planes = [scale_g, plane1]
         quantise(0, 0)
-        nc.vector.tensor_copy(keys[1][:], halves[:, 1, :])
         quantise(0, 1)
+
+        keys = []
+        for h in range(2):
+            word_g = sb.tile([P, HALF], U32, name="word_g%d" % h, tag="word_g%d" % h, align_bytes=64)
+            nc.vector.tensor_copy(word_g[:], word_win[:].indirect(offsets[:, h * HALF // 16:(h + 1) * HALF // 16]))
+            keys.append(sb.tile([P, PASSES, HALF], U16, name="keys%d" % h, align_bytes=64))
+            halves = word_g[:].bitcast(U16).rearrange("p (n g) -> p g n", g=PASSES)
+            if h == 0:
+                for g in range(PASSES):
+                    nc.vector.tensor_copy(keys[h][:, g], halves[:, g])
+            else:
+                nc.vector.tensor_copy(keys[h][:], halves)
+
+        cast(nc.scalar.copy, 1, 0, "grouped10")
+        cast(nc.scalar.copy, 1, 1, "grouped11")
         quantise(1, 0)
         quantise(1, 1)
 
-        dist = []
-        for m in range(TILES):
-            dist.append(sb.tile([P, N], F32, name="dist%d" % m, align_bytes=64))
-            nc.scalar.activation(dist[m][:], spread[:], ACT.Abs, bias=qpos[:, m:m + 1], scale=-1.0)
+        def multiply(acc, g, m, first):
+            h, inner = divmod(first, HALF)
+            nc.tensor.matmul_mx(
+                out=acc,
+                lhsT=codes[g, m][:].bitcast(FP8X4),
+                lhsT_scale=planes[g, m][:],
+                rhs=keys[h][:, g, inner:inner + P].bitcast(FP4X4),
+                rhs_scale=key_planes[g][:, first:first + P],
+                start=(g == 0),
+                stop=(g == PASSES - 1),
+            )
 
-        for m, first, count, width in ((0, 0, N, N), (1, 0, N // 2, P), (1, N // 2, N // 2, P)):
-            acc = psum.tile([P, count], F32, name="acc%d%d" % (m, first))
-            for n0 in range(0, count, width):
-                slots = slice(first + n0, first + n0 + width)
-                for g in range(PASSES):
-                    nc.tensor.matmul_mx(
-                        out=acc[:, n0:n0 + width],
-                        lhsT=codes[g, m][:].bitcast(FP8X4),
-                        lhsT_scale=planes[g, m][:],
-                        rhs=keys[g][:, slots].bitcast(FP4X4),
-                        rhs_scale=key_planes[g][:, slots],
-                        start=(g == 0),
-                        stop=(g == PASSES - 1),
-                    )
-            slots = slice(first, first + count)
-            result = sb.tile([P, count], F32, name="result%d%d" % (m, first), align_bytes=64)
+        def finish(acc, m, slots):
+            result = sb.tile([P, slots.stop - slots.start], F32, name="result%d_%d" % (m, slots.start), align_bytes=64)
             nc.vector.scalar_tensor_tensor(
-                result[:], dist[m][:, slots], neg_slope[:, m:m + 1], acc[:], ALU.mult, ALU.add
+                result[:], dist[m][:, slots], consts[:, TILES + m:TILES + m + 1], acc, ALU.mult, ALU.subtract,
+                reverse1=True,
             )
             nc.sync.dma_start(out[0, m * P:(m + 1) * P, slots], result[:])
+
+        early = {}
+        for m in range(TILES):
+            for first in (0, P):
+                early[m, first] = psum.tile([P, P], F32, name="early%d_%d" % (m, first))
+                multiply(early[m, first][:], 0, m, first)
+        for m in range(TILES):
+            for first in (0, P):
+                multiply(early[m, first][:], 1, m, first)
+                finish(early[m, first][:], m, slice(first, first + P))
+            width = HALF if m == 0 else P
+            for start in range(HALF, N, width):
+                tag = "turned" if start > HALF else "late%d" % m
+                late = psum.tile([P, width], F32, name="late%d_%d" % (m, start), tag=tag)
+                for first in range(start, start + width, P):
+                    for g in range(PASSES):
+                        multiply(late[:, first - start:first - start + P], g, m, first)
+                finish(late[:], m, slice(start, start + width))

@@ -49,8 +49,8 @@ def tile_attend_alibi_topk_kernel(tc, qT, k_words, k_scales, ps, sl, pq, offs, o
         scale_rows = k_scales.bitcast(I32).rearrange("o (q j) n -> j q o n", j=4)
         words = k_words[0].rearrange("p t b -> p (t b)").bitcast(I32)
 
-        nc.sync.dma_start(offsets[:], offs)
         nc.sync.dma_start(pos_win[LAST:P, :], ps[0:1, :])
+        nc.sync.dma_start(offsets[:], offs)
         nc.sync.dma_start(raw[0][:], q_rows[0])
         for j in range(4):
             nc.sync.dma_start(scale_win[j:P:16, :].bitcast(I32), scale_rows[j])
@@ -101,25 +101,26 @@ def tile_attend_alibi_topk_kernel(tc, qT, k_words, k_scales, ps, sl, pq, offs, o
 
         scale_g = sb.tile([P, N], U8, name="scale_g", align_bytes=64)
         nc.vector.tensor_copy(scale_g[:], scale_win[:].indirect(offsets[:]))
-        for first, count in ((32, 64), (0, 4), (96, 4)):
+        for first in range(0, P, 32):
             nc.sync.dma_start(
-                plane1[first:first + count, :].bitcast(I32), scale_g[first + 16:first + 16 + count, :].bitcast(I32)
+                plane1[first:first + 4, :].bitcast(I32), scale_g[first + 16:first + 20, :].bitcast(I32)
             )
         key_planes = [scale_g, plane1]
         quantise(0, 0)
         quantise(0, 1)
 
-        keys = []
+        parted = sb.tile([P, 2, PASSES, HALF], U16, name="parted", align_bytes=64)
+        keys = [parted[:, h] for h in range(2)]
+        word_g = sb.tile([P, N], U32, name="word_g", align_bytes=64)
+        halves = word_g[:].bitcast(U16).rearrange("p (h n g) -> p h g n", h=2, g=PASSES)
         for h in range(2):
-            word_g = sb.tile([P, HALF], U32, name="word_g%d" % h, tag="word_g%d" % h, align_bytes=64)
-            nc.vector.tensor_copy(word_g[:], word_win[:].indirect(offsets[:, h * HALF // 16:(h + 1) * HALF // 16]))
-            keys.append(sb.tile([P, PASSES, HALF], U16, name="keys%d" % h, align_bytes=64))
-            halves = word_g[:].bitcast(U16).rearrange("p (n g) -> p g n", g=PASSES)
-            if h == 0:
-                for g in range(PASSES):
-                    nc.vector.tensor_copy(keys[h][:, g], halves[:, g])
-            else:
-                nc.vector.tensor_copy(keys[h][:], halves)
+            nc.vector.tensor_copy(
+                word_g[:, h * HALF:(h + 1) * HALF],
+                word_win[:].indirect(offsets[:, h * HALF // 16:(h + 1) * HALF // 16]),
+            )
+        for h in range(2):
+            nc.vector.tensor_copy(parted[:, h, 0], halves[:, h, 0])
+        nc.vector.tensor_copy(parted[:, :, 1], halves[:, :, 1])
 
         cast(nc.scalar.copy, 1, 0, "grouped10")
         cast(nc.scalar.copy, 1, 1, "grouped11")
@@ -146,20 +147,15 @@ def tile_attend_alibi_topk_kernel(tc, qT, k_words, k_scales, ps, sl, pq, offs, o
             )
             nc.sync.dma_start(out[0, m * P:(m + 1) * P, slots], result[:])
 
-        early = {}
-        for m in range(TILES):
-            for first in (0, P):
-                early[m, first] = psum.tile([P, P], F32, name="early%d_%d" % (m, first))
-                multiply(early[m, first][:], 0, m, first)
-        for m in range(TILES):
-            for first in (0, P):
-                multiply(early[m, first][:], 1, m, first)
-                finish(early[m, first][:], m, slice(first, first + P))
-            width = HALF if m == 0 else P
-            for start in range(HALF, N, width):
-                tag = "turned" if start > HALF else "late%d" % m
-                late = psum.tile([P, width], F32, name="late%d_%d" % (m, start), tag=tag)
-                for first in range(start, start + width, P):
-                    for g in range(PASSES):
-                        multiply(late[:, first - start:first - start + P], g, m, first)
-                finish(late[:], m, slice(start, start + width))
+        banks = [psum.tile([P, P], F32, name="open%d" % c) for c in range(4)]
+        for g in range(PASSES):
+            for c in range(4):
+                multiply(banks[c][:], g, 0, c * P)
+                if g == PASSES - 1:
+                    finish(banks[c][:], 0, slice(c * P, (c + 1) * P))
+        for start, width, tag in ((0, HALF, "late0"), (HALF, P, "late1"), (HALF + P, P, "turned")):
+            late = psum.tile([P, width], F32, name="late%d" % start, tag=tag)
+            for first in range(start, start + width, P):
+                for g in range(PASSES):
+                    multiply(late[:, first - start:first - start + P], g, 1, first)
+            finish(late[:], 1, slice(start, start + width))

@@ -34,26 +34,25 @@ def tile_attend_alibi_topk_kernel(tc, qT, k_words, k_scales, ps, sl, pq, offs, o
         pos_win = sb.tile([P, T], F32, name="pos_win", align_bytes=64)
         scale_win = sb.tile([P, T], U8, name="scale_win", align_bytes=64)
         word_win = sb.tile([P, T], U32, name="word_win", align_bytes=64)
-        plane1 = sb.tile([P, N], U8, name="plane1", align_bytes=64)
+        key_planes = sb.tile([P, PASSES, N], U8, name="key_planes", align_bytes=64)
         ident = sb.tile([P, P], F32, name="ident", align_bytes=64)
         row_consts = sb.tile([P, P], F32, name="row_consts", align_bytes=64)
-        raw = [sb.tile([P, 4, NQ], F32, name="raw%d" % g, align_bytes=64) for g in range(PASSES)]
+        raw = [sb.tile([P, 4, NQ], F32, name="raw%d" % g, tag="raw%d" % g, align_bytes=64) for g in range(PASSES)]
 
         nc.vector.memset(scale_win[:].bitcast(I32), 0)
         nc.vector.memset(pos_win[0:LAST, :], 0.0)
-        make_identity(nc, ident[:])
-        nc.gpsimd.memset(plane1[:].bitcast(I32), 0)
         nc.gpsimd.memset(row_consts[0:ROWS, :], 0.0)
+        make_identity(nc, ident[:])
+        nc.gpsimd.memset(key_planes[:].rearrange("p g n -> p (g n)").bitcast(I32), 0)
 
         q_rows = qT[0].rearrange("(g p t) c -> g p t c", g=PASSES, t=4)
-        scale_rows = k_scales.bitcast(I32).rearrange("o (q j) n -> j q o n", j=4)
+        scale_rows = k_scales.bitcast(I32).rearrange("o f n -> f o n")
         words = k_words[0].rearrange("p t b -> p (t b)").bitcast(I32)
 
         nc.sync.dma_start(pos_win[LAST:P, :], ps[0:1, :])
         nc.sync.dma_start(offsets[:], offs)
         nc.sync.dma_start(raw[0][:], q_rows[0])
-        for j in range(4):
-            nc.sync.dma_start(scale_win[j:P:16, :].bitcast(I32), scale_rows[j])
+        nc.sync.dma_start(scale_win[0:P:4, :].bitcast(I32), scale_rows)
         nc.sync.dma_start(row_consts[ROWS:ROWS + TILES, :], pq[0].rearrange("(m p) o -> m (p o)", p=P))
         nc.sync.dma_start(row_consts[ROWS + TILES:P, :], sl[0].rearrange("(m p) o -> m (p o)", p=P))
         nc.sync.dma_start(word_win[:].bitcast(I32), words)
@@ -81,81 +80,76 @@ def tile_attend_alibi_topk_kernel(tc, qT, k_words, k_scales, ps, sl, pq, offs, o
 
         pos_g = sb.tile([P, N], F32, name="pos_g", align_bytes=64)
         nc.vector.tensor_copy(pos_g[:], pos_win[:].indirect(offsets[:]))
-        turned = psum.tile([P, 4, P], F32, name="turned", tag="turned")
+        turned = psum.tile([P, 4, P], F32, name="turned")
         for c in range(4):
             nc.tensor.transpose(turned[:, c, :], pos_g[:, c * P:(c + 1) * P], ident[:])
         cast(nc.scalar.copy, 0, 0, "grouped00")
         pos_col = sb.tile([P, 4], F32, name="pos_col")
         nc.scalar.copy(pos_col[:], turned[:, :, LAST])
         cast(nc.scalar.copy, 0, 1, "grouped01")
-        consts_t = psum.tile([P, P], F32, name="consts_t", tag="late1")
+        consts_t = psum.tile([P, P], F32, name="consts_t")
         nc.tensor.transpose(consts_t[:], row_consts[:], ident[:])
         consts = sb.tile([P, 2 * TILES], F32, name="consts")
         nc.scalar.copy(consts[:], consts_t[:, ROWS:P])
         spread = psum.tile([P, N], F32, name="spread")
         for c in range(4):
             nc.tensor.transpose(spread[:, c * P:(c + 1) * P], pos_col[:, c:c + 1].to_broadcast([P, P]), ident[:])
-        dist = [sb.tile([P, N], F32, name="dist%d" % m, align_bytes=64) for m in range(TILES)]
-        for m in range(TILES):
-            nc.scalar.activation(dist[m][:], spread[:], ACT.Abs, bias=consts[:, m:m + 1], scale=-1.0)
 
         scale_g = sb.tile([P, N], U8, name="scale_g", align_bytes=64)
         nc.vector.tensor_copy(scale_g[:], scale_win[:].indirect(offsets[:]))
         for first in range(0, P, 32):
-            nc.sync.dma_start(
-                plane1[first:first + 4, :].bitcast(I32), scale_g[first + 16:first + 20, :].bitcast(I32)
-            )
-        key_planes = [scale_g, plane1]
+            nc.sync.dma_start(key_planes[first:first + 4].bitcast(I32), scale_g[first:first + 32:4, :].bitcast(I32))
         quantise(0, 0)
         quantise(0, 1)
 
-        parted = sb.tile([P, 2, PASSES, HALF], U16, name="parted", align_bytes=64)
-        keys = [parted[:, h] for h in range(2)]
+        keys = sb.tile([P, PASSES, N], U16, name="keys", align_bytes=64)
         word_g = sb.tile([P, N], U32, name="word_g", align_bytes=64)
-        halves = word_g[:].bitcast(U16).rearrange("p (h n g) -> p h g n", h=2, g=PASSES)
+        pairs = word_g[:].bitcast(U16).rearrange("p (n g) -> p g n", g=PASSES)
         for h in range(2):
             nc.vector.tensor_copy(
                 word_g[:, h * HALF:(h + 1) * HALF],
                 word_win[:].indirect(offsets[:, h * HALF // 16:(h + 1) * HALF // 16]),
             )
         for h in range(2):
-            nc.vector.tensor_copy(parted[:, h, 0], halves[:, h, 0])
-        nc.vector.tensor_copy(parted[:, :, 1], halves[:, :, 1])
+            nc.vector.tensor_copy(keys[:, 0, h * HALF:(h + 1) * HALF], pairs[:, 0, h * HALF:(h + 1) * HALF])
+        nc.vector.tensor_copy(keys[:, 1, :], pairs[:, 1, :])
 
         cast(nc.scalar.copy, 1, 0, "grouped10")
         cast(nc.scalar.copy, 1, 1, "grouped11")
+        dist_all = sb.tile([P, TILES, N], F32, name="dist_all", tag="raw1", align_bytes=64)
+        dist = [dist_all[:, m] for m in range(TILES)]
+        for m, slots in ((0, slice(0, HALF)), (0, slice(HALF, N)), (1, slice(0, N))):
+            nc.scalar.activation(dist[m][:, slots], spread[:, slots], ACT.Abs, bias=consts[:, m:m + 1], scale=-1.0)
         quantise(1, 0)
         quantise(1, 1)
 
-        def multiply(acc, g, m, first):
-            h, inner = divmod(first, HALF)
-            nc.tensor.matmul_mx(
-                out=acc,
-                lhsT=codes[g, m][:].bitcast(FP8X4),
-                lhsT_scale=planes[g, m][:],
-                rhs=keys[h][:, g, inner:inner + P].bitcast(FP4X4),
-                rhs_scale=key_planes[g][:, first:first + P],
-                start=(g == 0),
-                stop=(g == PASSES - 1),
-            )
+        pieces = [(0, 0, HALF), (0, HALF, HALF), (1, 0, HALF), (1, HALF, P), (1, HALF + P, P)]
+        banks = [psum.tile([P, width], F32, name="bank%d" % i) for i, (m, start, width) in enumerate(pieces)]
 
-        def finish(acc, m, slots):
-            result = sb.tile([P, slots.stop - slots.start], F32, name="result%d_%d" % (m, slots.start), align_bytes=64)
+        def multiply(i, g):
+            m, start, width = pieces[i]
+            for first in range(start, start + width, P):
+                nc.tensor.matmul_mx(
+                    out=banks[i][:, first - start:first - start + P],
+                    lhsT=codes[g, m][:].bitcast(FP8X4),
+                    lhsT_scale=planes[g, m][:],
+                    rhs=keys[:, g, first:first + P].bitcast(FP4X4),
+                    rhs_scale=key_planes[:, g, first:first + P],
+                    start=(g == 0 and first == start),
+                    stop=(g == PASSES - 1 and first + P == start + width),
+                )
+
+        def finish(i):
+            m, start, width = pieces[i]
+            slots = slice(start, start + width)
+            result = sb.tile([P, width], F32, name="result%d" % i, align_bytes=64)
             nc.vector.scalar_tensor_tensor(
-                result[:], dist[m][:, slots], consts[:, TILES + m:TILES + m + 1], acc, ALU.mult, ALU.subtract,
+                result[:], dist[m][:, slots], consts[:, TILES + m:TILES + m + 1], banks[i][:], ALU.mult, ALU.subtract,
                 reverse1=True,
             )
             nc.sync.dma_start(out[0, m * P:(m + 1) * P, slots], result[:])
 
-        banks = [psum.tile([P, P], F32, name="open%d" % c) for c in range(4)]
-        for g in range(PASSES):
-            for c in range(4):
-                multiply(banks[c][:], g, 0, c * P)
-                if g == PASSES - 1:
-                    finish(banks[c][:], 0, slice(c * P, (c + 1) * P))
-        for start, width, tag in ((0, HALF, "late0"), (HALF, P, "late1"), (HALF + P, P, "turned")):
-            late = psum.tile([P, width], F32, name="late%d" % start, tag=tag)
-            for first in range(start, start + width, P):
-                for g in range(PASSES):
-                    multiply(late[:, first - start:first - start + P], g, 1, first)
-            finish(late[:], 1, slice(start, start + width))
+        for i, g in ((0, 0), (1, 0), (2, 0), (0, 1), (1, 1), (2, 1), (3, 0), (3, 1), (4, 0), (4, 1)):
+            multiply(i, g)
+            if g == PASSES - 1:
+                finish(i)

@@ -32,15 +32,15 @@ def tile_attend_alibi_topk_kernel(tc, qT, k_words, k_scales, ps, sl, pq, offs, o
 
         offsets = sb.tile([P, N // 16], U16, name="offsets")
         pos_win = sb.tile([P, T], F32, name="pos_win", align_bytes=64)
-        scale_win = sb.tile([P, T], U8, name="scale_win", align_bytes=64)
+        scale_win = sb.tile([P, T], U8, name="scale_win", tag="scale_win", align_bytes=64)
         word_win = sb.tile([P, T], U32, name="word_win", align_bytes=64)
         key_planes = sb.tile([P, PASSES, N], U8, name="key_planes", align_bytes=64)
         ident = sb.tile([P, P], F32, name="ident", align_bytes=64)
         row_consts = sb.tile([P, P], F32, name="row_consts", align_bytes=64)
         raw = [sb.tile([P, 4, NQ], F32, name="raw%d" % g, tag="raw%d" % g, align_bytes=64) for g in range(PASSES)]
 
-        nc.vector.memset(scale_win[:].bitcast(I32), 0)
         nc.vector.memset(pos_win[0:LAST, :], 0.0)
+        nc.vector.memset(scale_win[0:96, :].bitcast(I32), 0)
         nc.gpsimd.memset(row_consts[0:ROWS, :], 0.0)
         make_identity(nc, ident[:])
         nc.gpsimd.memset(key_planes[:].rearrange("p g n -> p (g n)").bitcast(I32), 0)
@@ -51,8 +51,8 @@ def tile_attend_alibi_topk_kernel(tc, qT, k_words, k_scales, ps, sl, pq, offs, o
 
         nc.sync.dma_start(pos_win[LAST:P, :], ps[0:1, :])
         nc.sync.dma_start(offsets[:], offs)
+        nc.sync.dma_start(scale_win[96:P, :].bitcast(I32), scale_rows)
         nc.sync.dma_start(raw[0][:], q_rows[0])
-        nc.sync.dma_start(scale_win[0:P:4, :].bitcast(I32), scale_rows)
         nc.sync.dma_start(row_consts[ROWS:ROWS + TILES, :], pq[0].rearrange("(m p) o -> m (p o)", p=P))
         nc.sync.dma_start(row_consts[ROWS + TILES:P, :], sl[0].rearrange("(m p) o -> m (p o)", p=P))
         nc.sync.dma_start(word_win[:].bitcast(I32), words)
@@ -78,11 +78,22 @@ def tile_attend_alibi_topk_kernel(tc, qT, k_words, k_scales, ps, sl, pq, offs, o
                 in_=grouped[g, m][:].rearrange("p c t -> p (c t)"),
             )
 
-        pos_g = sb.tile([P, N], F32, name="pos_g", align_bytes=64)
-        nc.vector.tensor_copy(pos_g[:], pos_win[:].indirect(offsets[:]))
         turned = psum.tile([P, 4, P], F32, name="turned")
-        for c in range(4):
-            nc.tensor.transpose(turned[:, c, :], pos_g[:, c * P:(c + 1) * P], ident[:])
+
+        def positions(h, tag):
+            pos_g = sb.tile([P, HALF], F32, name="pos_g%d" % h, tag=tag, align_bytes=64)
+            nc.vector.tensor_copy(pos_g[:], pos_win[:].indirect(offsets[:, h * HALF // 16:(h + 1) * HALF // 16]))
+            for c in range(2):
+                nc.tensor.transpose(turned[:, 2 * h + c, :], pos_g[:, c * P:(c + 1) * P], ident[:])
+
+        positions(0, "pos_g0")
+        scale_g = sb.tile([P, N], U8, name="scale_g", align_bytes=64)
+        nc.vector.tensor_copy(scale_g[:], scale_win[:].indirect(offsets[:]))
+        for q in range(4):
+            nc.sync.dma_start(
+                key_planes[32 * q:32 * q + 4].bitcast(I32), scale_g[96 + 8 * q:96 + 8 * q + 8, :].bitcast(I32)
+            )
+        positions(1, "scale_win")
         cast(nc.scalar.copy, 0, 0, "grouped00")
         pos_col = sb.tile([P, 4], F32, name="pos_col")
         nc.scalar.copy(pos_col[:], turned[:, :, LAST])
@@ -95,10 +106,6 @@ def tile_attend_alibi_topk_kernel(tc, qT, k_words, k_scales, ps, sl, pq, offs, o
         for c in range(4):
             nc.tensor.transpose(spread[:, c * P:(c + 1) * P], pos_col[:, c:c + 1].to_broadcast([P, P]), ident[:])
 
-        scale_g = sb.tile([P, N], U8, name="scale_g", align_bytes=64)
-        nc.vector.tensor_copy(scale_g[:], scale_win[:].indirect(offsets[:]))
-        for first in range(0, P, 32):
-            nc.sync.dma_start(key_planes[first:first + 4].bitcast(I32), scale_g[first:first + 32:4, :].bitcast(I32))
         quantise(0, 0)
         quantise(0, 1)
 
@@ -118,8 +125,9 @@ def tile_attend_alibi_topk_kernel(tc, qT, k_words, k_scales, ps, sl, pq, offs, o
         cast(nc.scalar.copy, 1, 1, "grouped11")
         dist_all = sb.tile([P, TILES, N], F32, name="dist_all", tag="raw1", align_bytes=64)
         dist = [dist_all[:, m] for m in range(TILES)]
-        for m, slots in ((0, slice(0, HALF)), (0, slice(HALF, N)), (1, slice(0, N))):
-            nc.scalar.activation(dist[m][:, slots], spread[:, slots], ACT.Abs, bias=consts[:, m:m + 1], scale=-1.0)
+        for m in range(TILES):
+            for slots in (slice(0, HALF), slice(HALF, N)):
+                nc.scalar.activation(dist[m][:, slots], spread[:, slots], ACT.Abs, bias=consts[:, m:m + 1], scale=-1.0)
         quantise(1, 0)
         quantise(1, 1)
 

@@ -29,19 +29,22 @@ def tile_attend_alibi_topk_kernel(tc, qT, k_words, k_scales, ps, sl, pq, offs, o
         LAST = P - 1
         ROWS = P - 2 * TILES
         HALF = N // 2
+        SHARE = 40
 
         offsets = sb.tile([P, N // 16], U16, name="offsets")
         pos_win = sb.tile([P, T], F32, name="pos_win", align_bytes=64)
-        scale_win = sb.tile([P, T], U8, name="scale_win", tag="scale_win", align_bytes=64)
+        scale_win = sb.tile([P, T], U8, name="scale_win", tag="late", align_bytes=64)
         word_win = sb.tile([P, T], U32, name="word_win", align_bytes=64)
         key_planes = sb.tile([P, PASSES, N], U8, name="key_planes", align_bytes=64)
         ident = sb.tile([P, P], F32, name="ident", align_bytes=64)
+        zero = sb.tile([P, 1], F32, name="zero")
         row_consts = sb.tile([P, P], F32, name="row_consts", align_bytes=64)
-        raw = [sb.tile([P, 4, NQ], F32, name="raw%d" % g, tag="raw%d" % g, align_bytes=64) for g in range(PASSES)]
+        raw0 = sb.tile([P, 4, NQ], F32, name="raw0", align_bytes=64)
+        raw1 = [sb.tile([P, 2, NQ], F32, name="raw10", tag="raw10", align_bytes=64)]
 
-        nc.vector.memset(pos_win[0:LAST, :], 0.0)
+        nc.gpsimd.memset(zero[:], 0.0)
         nc.vector.memset(scale_win[0:96, :].bitcast(I32), 0)
-        nc.gpsimd.memset(row_consts[0:ROWS, :], 0.0)
+        nc.vector.memset(pos_win[0:LAST, :], 0.0)
         make_identity(nc, ident[:])
         nc.gpsimd.memset(key_planes[:].rearrange("p g n -> p (g n)").bitcast(I32), 0)
 
@@ -49,24 +52,70 @@ def tile_attend_alibi_topk_kernel(tc, qT, k_words, k_scales, ps, sl, pq, offs, o
         scale_rows = k_scales.bitcast(I32).rearrange("o f n -> f o n")
         words = k_words[0].rearrange("p t b -> p (t b)").bitcast(I32)
 
-        nc.sync.dma_start(pos_win[LAST:P, :], ps[0:1, :])
         nc.sync.dma_start(offsets[:], offs)
         nc.sync.dma_start(scale_win[96:P, :].bitcast(I32), scale_rows)
-        nc.sync.dma_start(raw[0][:], q_rows[0])
-        nc.sync.dma_start(row_consts[ROWS:ROWS + TILES, :], pq[0].rearrange("(m p) o -> m (p o)", p=P))
-        nc.sync.dma_start(row_consts[ROWS + TILES:P, :], sl[0].rearrange("(m p) o -> m (p o)", p=P))
+        nc.sync.dma_start(pos_win[LAST:P, :], ps[0:1, :])
         nc.sync.dma_start(word_win[:].bitcast(I32), words)
-        nc.sync.dma_start(raw[1][:], q_rows[1])
+        nc.sync.dma_start(raw0[:], q_rows[0])
+        nc.sync.dma_start(raw1[0][:], q_rows[1][:, 0:2])
+        nc.scalar.dma_start(row_consts[ROWS:ROWS + TILES, :], pq[0].rearrange("(m p) o -> m (p o)", p=P))
+        nc.scalar.dma_start(row_consts[ROWS + TILES:P, :], sl[0].rearrange("(m p) o -> m (p o)", p=P))
+        nc.scalar.copy(row_consts[0:ROWS, :], zero[0:ROWS, :].to_broadcast([ROWS, P]))
+
+        def listed(window, first, count):
+            return window[:].indirect(offsets[:, first // 16:(first + count) // 16])
+
+        turned = psum.tile([P, 4, P], F32, name="turned", tag="turned")
+        pos_g = [sb.tile([P, HALF], F32, name="pos_g%d" % h, align_bytes=64) for h in range(2)]
+        for h in range(2):
+            nc.scalar.activation(pos_g[h][:], listed(pos_win, h * HALF, HALF), ACT.Copy)
+            for c in range(2):
+                nc.tensor.transpose(turned[:, 2 * h + c, :], pos_g[h][:, c * P:(c + 1) * P], ident[:])
+
+        scale_g = sb.tile([P, N], U8, name="scale_g", align_bytes=64)
+        nc.vector.tensor_copy(scale_g[:], listed(scale_win, 0, N))
+        for q in range(4):
+            nc.sync.dma_start(
+                key_planes[32 * q:32 * q + 4].bitcast(I32), scale_g[96 + 8 * q:96 + 8 * q + 8, :].bitcast(I32)
+            )
+        raw1.append(sb.tile([P, 2, NQ], F32, name="raw11", tag="late", align_bytes=64))
+        nc.sync.dma_start(raw1[1][:], q_rows[1][:, 2:4])
+
+        pos_col = sb.tile([P, 4], F32, name="pos_col")
+        nc.scalar.copy(pos_col[:], turned[:, :, LAST])
+        consts_t = psum.tile([P, P], F32, name="consts_t", tag="turned")
+        nc.tensor.transpose(consts_t[:], row_consts[:], ident[:])
+        consts = sb.tile([P, 2 * TILES], F32, name="consts")
+        nc.scalar.copy(consts[:], consts_t[:, ROWS:P])
+        spread = psum.tile([P, N], F32, name="spread")
+        for c in range(4):
+            nc.tensor.transpose(spread[:, c * P:(c + 1) * P], pos_col[:, c:c + 1].to_broadcast([P, P]), ident[:])
+
+        word_g = sb.tile([P, N], U32, name="word_g", align_bytes=64)
+        pairs = word_g[:].bitcast(U16).rearrange("p (n g) -> p g n", g=PASSES)
+        keys = {}
+        for h in range(2):
+            nc.vector.tensor_copy(word_g[:, h * HALF:(h + 1) * HALF], listed(word_win, h * HALF, HALF))
 
         codes = {}
         planes = {}
         grouped = {}
 
-        def cast(copy, g, m, tag):
-            grouped[g, m] = sb.tile([P, P, 4], BF16, name="grouped%d%d" % (g, m), tag=tag, align_bytes=64)
+        for g in range(PASSES):
+            for m in range(TILES):
+                name = "grouped%d%d" % (g, m)
+                grouped[g, m] = sb.tile([P, P, 4], BF16, name=name, tag=name, align_bytes=64)
+
+        def cast0(copy, m, first, end):
             copy(
-                grouped[g, m][:].rearrange("p (c i) t -> p c t i", i=4),
-                raw[g][:, :, m * P:(m + 1) * P].rearrange("p t (c i) -> p c t i", i=4),
+                grouped[0, m][:, first:end, :].rearrange("p (c i) t -> p c t i", i=4),
+                raw0[:, :, m * P + first:m * P + end].rearrange("p t (c i) -> p c t i", i=4),
+            )
+
+        def cast1(copy, m, u):
+            copy(
+                grouped[1, m][:, :, 2 * u:2 * u + 2].rearrange("p (c i) t -> p c t i", i=4),
+                raw1[u][:, :, m * P:(m + 1) * P].rearrange("p t (c i) -> p c t i", i=4),
             )
 
         def quantise(g, m):
@@ -78,74 +127,46 @@ def tile_attend_alibi_topk_kernel(tc, qT, k_words, k_scales, ps, sl, pq, offs, o
                 in_=grouped[g, m][:].rearrange("p c t -> p (c t)"),
             )
 
-        turned = psum.tile([P, 4, P], F32, name="turned")
+        def part(g, h, tag):
+            keys[g, h] = sb.tile([P, HALF], U16, name="keys%d%d" % (g, h), tag=tag, align_bytes=64)
+            nc.vector.tensor_copy(keys[g, h][:], pairs[:, g, h * HALF:(h + 1) * HALF])
 
-        def positions(h, tag):
-            pos_g = sb.tile([P, HALF], F32, name="pos_g%d" % h, tag=tag, align_bytes=64)
-            nc.vector.tensor_copy(pos_g[:], pos_win[:].indirect(offsets[:, h * HALF // 16:(h + 1) * HALF // 16]))
-            for c in range(2):
-                nc.tensor.transpose(turned[:, 2 * h + c, :], pos_g[:, c * P:(c + 1) * P], ident[:])
-
-        positions(0, "pos_g0")
-        scale_g = sb.tile([P, N], U8, name="scale_g", align_bytes=64)
-        nc.vector.tensor_copy(scale_g[:], scale_win[:].indirect(offsets[:]))
-        for q in range(4):
-            nc.sync.dma_start(
-                key_planes[32 * q:32 * q + 4].bitcast(I32), scale_g[96 + 8 * q:96 + 8 * q + 8, :].bitcast(I32)
-            )
-        positions(1, "scale_win")
-        cast(nc.scalar.copy, 0, 0, "grouped00")
-        pos_col = sb.tile([P, 4], F32, name="pos_col")
-        nc.scalar.copy(pos_col[:], turned[:, :, LAST])
-        cast(nc.scalar.copy, 0, 1, "grouped01")
-        consts_t = psum.tile([P, P], F32, name="consts_t")
-        nc.tensor.transpose(consts_t[:], row_consts[:], ident[:])
-        consts = sb.tile([P, 2 * TILES], F32, name="consts")
-        nc.scalar.copy(consts[:], consts_t[:, ROWS:P])
-        spread = psum.tile([P, N], F32, name="spread")
-        for c in range(4):
-            nc.tensor.transpose(spread[:, c * P:(c + 1) * P], pos_col[:, c:c + 1].to_broadcast([P, P]), ident[:])
-
+        part(0, 0, "keys00")
+        part(0, 1, "keys01")
+        cast0(nc.scalar.copy, 0, SHARE, P)
+        cast0(nc.vector.tensor_copy, 0, 0, SHARE)
         quantise(0, 0)
+        cast0(nc.scalar.copy, 1, 0, P)
+        part(1, 0, "grouped00")
         quantise(0, 1)
+        cast1(nc.scalar.copy, 0, 0)
+        cast1(nc.scalar.copy, 1, 0)
+        cast1(nc.vector.tensor_copy, 0, 1)
+        part(1, 1, "grouped01")
+        quantise(1, 0)
+        cast1(nc.vector.tensor_copy, 1, 1)
+        quantise(1, 1)
 
-        keys = sb.tile([P, PASSES, N], U16, name="keys", align_bytes=64)
-        word_g = sb.tile([P, N], U32, name="word_g", align_bytes=64)
-        pairs = word_g[:].bitcast(U16).rearrange("p (n g) -> p g n", g=PASSES)
-        for h in range(2):
-            nc.vector.tensor_copy(
-                word_g[:, h * HALF:(h + 1) * HALF],
-                word_win[:].indirect(offsets[:, h * HALF // 16:(h + 1) * HALF // 16]),
-            )
-        for h in range(2):
-            nc.vector.tensor_copy(keys[:, 0, h * HALF:(h + 1) * HALF], pairs[:, 0, h * HALF:(h + 1) * HALF])
-        nc.vector.tensor_copy(keys[:, 1, :], pairs[:, 1, :])
-
-        cast(nc.scalar.copy, 1, 0, "grouped10")
-        cast(nc.scalar.copy, 1, 1, "grouped11")
-        dist_all = sb.tile([P, TILES, N], F32, name="dist_all", tag="raw1", align_bytes=64)
+        dist_all = sb.tile([P, TILES, N], F32, name="dist_all", tag="raw10", align_bytes=64)
         dist = [dist_all[:, m] for m in range(TILES)]
         for m in range(TILES):
             for slots in (slice(0, HALF), slice(HALF, N)):
                 nc.scalar.activation(dist[m][:, slots], spread[:, slots], ACT.Abs, bias=consts[:, m:m + 1], scale=-1.0)
-        quantise(1, 0)
-        quantise(1, 1)
 
         pieces = [(0, 0, HALF), (0, HALF, HALF), (1, 0, HALF), (1, HALF, P), (1, HALF + P, P)]
         banks = [psum.tile([P, width], F32, name="bank%d" % i) for i, (m, start, width) in enumerate(pieces)]
 
         def multiply(i, g):
             m, start, width = pieces[i]
-            for first in range(start, start + width, P):
-                nc.tensor.matmul_mx(
-                    out=banks[i][:, first - start:first - start + P],
-                    lhsT=codes[g, m][:].bitcast(FP8X4),
-                    lhsT_scale=planes[g, m][:],
-                    rhs=keys[:, g, first:first + P].bitcast(FP4X4),
-                    rhs_scale=key_planes[:, g, first:first + P],
-                    start=(g == 0 and first == start),
-                    stop=(g == PASSES - 1 and first + P == start + width),
-                )
+            nc.tensor.matmul_mx(
+                out=banks[i][:],
+                lhsT=codes[g, m][:].bitcast(FP8X4),
+                lhsT_scale=planes[g, m][:],
+                rhs=keys[g, start // HALF][:, start % HALF:start % HALF + width].bitcast(FP4X4),
+                rhs_scale=key_planes[:, g, start:start + width],
+                start=(g == 0),
+                stop=(g == PASSES - 1),
+            )
 
         def finish(i):
             m, start, width = pieces[i]
@@ -157,7 +178,8 @@ def tile_attend_alibi_topk_kernel(tc, qT, k_words, k_scales, ps, sl, pq, offs, o
             )
             nc.sync.dma_start(out[0, m * P:(m + 1) * P, slots], result[:])
 
-        for i, g in ((0, 0), (1, 0), (2, 0), (0, 1), (1, 1), (2, 1), (3, 0), (3, 1), (4, 0), (4, 1)):
-            multiply(i, g)
-            if g == PASSES - 1:
-                finish(i)
+        for i in range(len(pieces)):
+            multiply(i, 0)
+        for i in range(len(pieces)):
+            multiply(i, 1)
+            finish(i)

@@ -29,22 +29,21 @@ def tile_attend_alibi_topk_kernel(tc, qT, k_words, k_scales, ps, sl, pq, offs, o
         LAST = P - 1
         ROWS = P - 2 * TILES
         HALF = N // 2
-        SHARE = 40
+        SHARE = 72
 
         offsets = sb.tile([P, N // 16], U16, name="offsets")
         pos_win = sb.tile([P, T], F32, name="pos_win", align_bytes=64)
-        scale_win = sb.tile([P, T], U8, name="scale_win", tag="late", align_bytes=64)
+        scale_win = sb.tile([P, T], U8, name="scale_win", align_bytes=64)
         word_win = sb.tile([P, T], U32, name="word_win", align_bytes=64)
         key_planes = sb.tile([P, PASSES, N], U8, name="key_planes", align_bytes=64)
         ident = sb.tile([P, P], F32, name="ident", align_bytes=64)
         zero = sb.tile([P, 1], F32, name="zero")
         row_consts = sb.tile([P, P], F32, name="row_consts", align_bytes=64)
-        raw0 = sb.tile([P, 4, NQ], F32, name="raw0", align_bytes=64)
-        raw1 = [sb.tile([P, 2, NQ], F32, name="raw10", tag="raw10", align_bytes=64)]
+        raw = [sb.tile([P, 4, NQ], F32, name="raw%d" % g, tag="raw%d" % g, align_bytes=64) for g in range(PASSES)]
 
         nc.gpsimd.memset(zero[:], 0.0)
-        nc.vector.memset(scale_win[0:96, :].bitcast(I32), 0)
         nc.vector.memset(pos_win[0:LAST, :], 0.0)
+        nc.vector.memset(scale_win[0:96, :].bitcast(I32), 0)
         make_identity(nc, ident[:])
         nc.gpsimd.memset(key_planes[:].rearrange("p g n -> p (g n)").bitcast(I32), 0)
 
@@ -52,23 +51,23 @@ def tile_attend_alibi_topk_kernel(tc, qT, k_words, k_scales, ps, sl, pq, offs, o
         scale_rows = k_scales.bitcast(I32).rearrange("o f n -> f o n")
         words = k_words[0].rearrange("p t b -> p (t b)").bitcast(I32)
 
+        nc.scalar.dma_start(row_consts[ROWS:ROWS + TILES, :], pq[0].rearrange("(m p) o -> m (p o)", p=P))
+        nc.scalar.dma_start(row_consts[ROWS + TILES:P, :], sl[0].rearrange("(m p) o -> m (p o)", p=P))
+        nc.scalar.copy(row_consts[0:ROWS, :], zero[0:ROWS, :].to_broadcast([ROWS, P]))
         nc.sync.dma_start(offsets[:], offs)
         nc.sync.dma_start(scale_win[96:P, :].bitcast(I32), scale_rows)
         nc.sync.dma_start(pos_win[LAST:P, :], ps[0:1, :])
         nc.sync.dma_start(word_win[:].bitcast(I32), words)
-        nc.sync.dma_start(raw0[:], q_rows[0])
-        nc.sync.dma_start(raw1[0][:], q_rows[1][:, 0:2])
-        nc.scalar.dma_start(row_consts[ROWS:ROWS + TILES, :], pq[0].rearrange("(m p) o -> m (p o)", p=P))
-        nc.scalar.dma_start(row_consts[ROWS + TILES:P, :], sl[0].rearrange("(m p) o -> m (p o)", p=P))
-        nc.scalar.copy(row_consts[0:ROWS, :], zero[0:ROWS, :].to_broadcast([ROWS, P]))
+        nc.sync.dma_start(raw[0][:], q_rows[0])
+        nc.sync.dma_start(raw[1][:, 0:3], q_rows[1][:, 0:3])
 
         def listed(window, first, count):
             return window[:].indirect(offsets[:, first // 16:(first + count) // 16])
 
         turned = psum.tile([P, 4, P], F32, name="turned", tag="turned")
-        pos_g = [sb.tile([P, HALF], F32, name="pos_g%d" % h, align_bytes=64) for h in range(2)]
+        pos_g = [raw[1][:, 3], sb.tile([P, HALF], F32, name="pos_g1", tag="early", align_bytes=64)[:]]
         for h in range(2):
-            nc.scalar.activation(pos_g[h][:], listed(pos_win, h * HALF, HALF), ACT.Copy)
+            nc.scalar.activation(pos_g[h], listed(pos_win, h * HALF, HALF), ACT.Copy)
             for c in range(2):
                 nc.tensor.transpose(turned[:, 2 * h + c, :], pos_g[h][:, c * P:(c + 1) * P], ident[:])
 
@@ -78,8 +77,7 @@ def tile_attend_alibi_topk_kernel(tc, qT, k_words, k_scales, ps, sl, pq, offs, o
             nc.sync.dma_start(
                 key_planes[32 * q:32 * q + 4].bitcast(I32), scale_g[96 + 8 * q:96 + 8 * q + 8, :].bitcast(I32)
             )
-        raw1.append(sb.tile([P, 2, NQ], F32, name="raw11", tag="late", align_bytes=64))
-        nc.sync.dma_start(raw1[1][:], q_rows[1][:, 2:4])
+        nc.sync.dma_start(raw[1][:, 3], q_rows[1][:, 3])
 
         pos_col = sb.tile([P, 4], F32, name="pos_col")
         nc.scalar.copy(pos_col[:], turned[:, :, LAST])
@@ -93,29 +91,18 @@ def tile_attend_alibi_topk_kernel(tc, qT, k_words, k_scales, ps, sl, pq, offs, o
 
         word_g = sb.tile([P, N], U32, name="word_g", align_bytes=64)
         pairs = word_g[:].bitcast(U16).rearrange("p (n g) -> p g n", g=PASSES)
-        keys = {}
         for h in range(2):
             nc.vector.tensor_copy(word_g[:, h * HALF:(h + 1) * HALF], listed(word_win, h * HALF, HALF))
 
+        keys = {}
         codes = {}
         planes = {}
         grouped = {}
 
-        for g in range(PASSES):
-            for m in range(TILES):
-                name = "grouped%d%d" % (g, m)
-                grouped[g, m] = sb.tile([P, P, 4], BF16, name=name, tag=name, align_bytes=64)
-
-        def cast0(copy, m, first, end):
+        def cast(copy, g, m, first, end):
             copy(
-                grouped[0, m][:, first:end, :].rearrange("p (c i) t -> p c t i", i=4),
-                raw0[:, :, m * P + first:m * P + end].rearrange("p t (c i) -> p c t i", i=4),
-            )
-
-        def cast1(copy, m, u):
-            copy(
-                grouped[1, m][:, :, 2 * u:2 * u + 2].rearrange("p (c i) t -> p c t i", i=4),
-                raw1[u][:, :, m * P:(m + 1) * P].rearrange("p t (c i) -> p c t i", i=4),
+                grouped[g, m][:, first:end, :].rearrange("p (c i) t -> p c t i", i=4),
+                raw[g][:, :, m * P + first:m * P + end].rearrange("p t (c i) -> p c t i", i=4),
             )
 
         def quantise(g, m):
@@ -124,37 +111,43 @@ def tile_attend_alibi_topk_kernel(tc, qT, k_words, k_scales, ps, sl, pq, offs, o
             nc.vector.quantize_mx(
                 out=codes[g, m][:].bitcast(FP8X4),
                 scales=planes[g, m][:],
-                in_=grouped[g, m][:].rearrange("p c t -> p (c t)"),
+                in_=grouped[g, m].rearrange("p c t -> p (c t)"),
             )
 
         def part(g, h, tag):
             keys[g, h] = sb.tile([P, HALF], U16, name="keys%d%d" % (g, h), tag=tag, align_bytes=64)
             nc.vector.tensor_copy(keys[g, h][:], pairs[:, g, h * HALF:(h + 1) * HALF])
 
+        grouped0 = sb.tile([P, TILES, P, 4], BF16, name="grouped0", tag="early", align_bytes=64)
+        for m in range(TILES):
+            grouped[0, m] = grouped0[:, m]
+            grouped[1, m] = sb.tile([P, P, 4], BF16, name="grouped1%d" % m, tag="grouped1%d" % m, align_bytes=64)[:]
+
         part(0, 0, "keys00")
         part(0, 1, "keys01")
-        cast0(nc.scalar.copy, 0, SHARE, P)
-        cast0(nc.vector.tensor_copy, 0, 0, SHARE)
+        part(1, 0, "keys10")
+        cast(nc.scalar.copy, 0, 0, 0, P)
         quantise(0, 0)
-        cast0(nc.scalar.copy, 1, 0, P)
-        part(1, 0, "grouped00")
+        cast(nc.scalar.copy, 0, 1, 0, P)
         quantise(0, 1)
-        cast1(nc.scalar.copy, 0, 0)
-        cast1(nc.scalar.copy, 1, 0)
-        cast1(nc.vector.tensor_copy, 0, 1)
-        part(1, 1, "grouped01")
+        cast(nc.scalar.copy, 1, 0, SHARE, P)
+        cast(nc.vector.tensor_copy, 1, 0, 0, SHARE)
+        part(1, 1, "early")
         quantise(1, 0)
-        cast1(nc.vector.tensor_copy, 1, 1)
+        cast(nc.scalar.copy, 1, 1, 0, P)
         quantise(1, 1)
 
-        dist_all = sb.tile([P, TILES, N], F32, name="dist_all", tag="raw10", align_bytes=64)
+        dist_all = sb.tile([P, TILES, N], F32, name="dist_all", tag="raw1", align_bytes=64)
         dist = [dist_all[:, m] for m in range(TILES)]
         for m in range(TILES):
             for slots in (slice(0, HALF), slice(HALF, N)):
                 nc.scalar.activation(dist[m][:, slots], spread[:, slots], ACT.Abs, bias=consts[:, m:m + 1], scale=-1.0)
 
-        pieces = [(0, 0, HALF), (0, HALF, HALF), (1, 0, HALF), (1, HALF, P), (1, HALF + P, P)]
-        banks = [psum.tile([P, width], F32, name="bank%d" % i) for i, (m, start, width) in enumerate(pieces)]
+        pieces = [(0, 0, P), (0, P, P), (0, HALF, HALF), (1, 0, HALF), (1, HALF, P), (1, HALF + P, P)]
+        banks = [
+            psum.tile([P, width], F32, name="bank%d" % i, tag="turned" if i == len(pieces) - 1 else "bank%d" % i)
+            for i, (m, start, width) in enumerate(pieces)
+        ]
 
         def multiply(i, g):
             m, start, width = pieces[i]
@@ -178,8 +171,10 @@ def tile_attend_alibi_topk_kernel(tc, qT, k_words, k_scales, ps, sl, pq, offs, o
             )
             nc.sync.dma_start(out[0, m * P:(m + 1) * P, slots], result[:])
 
-        for i in range(len(pieces)):
+        for i in range(4):
             multiply(i, 0)
         for i in range(len(pieces)):
+            if i >= 4:
+                multiply(i, 0)
             multiply(i, 1)
             finish(i)

@@ -59,13 +59,13 @@ def tile_attend_alibi_topk_kernel(tc, qT, k_words, k_scales, ps, sl, pq, offs, o
         nc.sync.dma_start(pos_win[LAST:P, :], ps[0:1, :])
         nc.sync.dma_start(word_win[:].bitcast(I32), words)
         nc.sync.dma_start(raw[0][:], q_rows[0])
-        nc.sync.dma_start(raw[1][:, 0:3], q_rows[1][:, 0:3])
+        nc.sync.dma_start(raw[1][:], q_rows[1])
 
         def listed(window, first, count):
             return window[:].indirect(offsets[:, first // 16:(first + count) // 16])
 
         turned = psum.tile([P, 4, P], F32, name="turned", tag="turned")
-        pos_g = [raw[1][:, 3], sb.tile([P, HALF], F32, name="pos_g1", tag="early", align_bytes=64)[:]]
+        pos_g = [sb.tile([P, HALF], F32, name="pos_g0", align_bytes=64)[:], sb.tile([P, HALF], F32, name="pos_g1", tag="early", align_bytes=64)[:]]
         for h in range(2):
             nc.scalar.activation(pos_g[h], listed(pos_win, h * HALF, HALF), ACT.Copy)
             for c in range(2):
@@ -77,7 +77,6 @@ def tile_attend_alibi_topk_kernel(tc, qT, k_words, k_scales, ps, sl, pq, offs, o
             nc.sync.dma_start(
                 key_planes[32 * q:32 * q + 4].bitcast(I32), scale_g[96 + 8 * q:96 + 8 * q + 8, :].bitcast(I32)
             )
-        nc.sync.dma_start(raw[1][:, 3], q_rows[1][:, 3])
 
         pos_col = sb.tile([P, 4], F32, name="pos_col")
         nc.scalar.copy(pos_col[:], turned[:, :, LAST])

@@ -160,20 +160,28 @@ def tile_attend_alibi_topk_kernel(tc, qT, k_words, k_scales, ps, sl, pq, offs, o
                 stop=(g == PASSES - 1),
             )
 
+        results = sb.tile([P, TILES, N], F32, name="results", align_bytes=64)
+
         def finish(i):
             m, start, width = pieces[i]
             slots = slice(start, start + width)
-            result = sb.tile([P, width], F32, name="result%d" % i, align_bytes=64)
             nc.vector.scalar_tensor_tensor(
-                result[:], dist[m][:, slots], consts[:, TILES + m:TILES + m + 1], banks[i][:], ALU.mult, ALU.subtract,
-                reverse1=True,
+                results[:, m, slots], dist[m][:, slots], consts[:, TILES + m:TILES + m + 1], banks[i][:],
+                ALU.mult, ALU.subtract, reverse1=True,
             )
-            nc.sync.dma_start(out[0, m * P:(m + 1) * P, slots], result[:])
 
-        for i in range(4):
+        def store(first, last):
+            m = pieces[first][0]
+            slots = slice(pieces[first][1], pieces[last][1] + pieces[last][2])
+            nc.sync.dma_start(out[0, m * P:(m + 1) * P, slots], results[:, m, slots])
+
+        for i in range(3):
             multiply(i, 0)
         for i in range(len(pieces)):
-            if i >= 4:
+            if i >= 3:
                 multiply(i, 0)
             multiply(i, 1)
             finish(i)
+            if i < 4:
+                store(i, i)
+        store(4, 5)

@@ -27,9 +27,10 @@ def tile_attend_alibi_topk_kernel(tc, qT, k_words, k_scales, ps, sl, pq, offs, o
         sb = ctx.enter_context(tc.tile_pool(name="sb", bufs=1))
         psum = ctx.enter_context(tc.psum_pool(name="psum", bufs=1))
         LAST = P - 1
-        ROWS = P - 2 * TILES
+        ROWS = 96 - 2 * TILES
         HALF = N // 2
-        SHARE = 72
+        AHEAD = T // 8
+        SHARE = 96
 
         offsets = sb.tile([P, N // 16], U16, name="offsets")
         pos_win = sb.tile([P, T], F32, name="pos_win", align_bytes=64)
@@ -42,8 +43,10 @@ def tile_attend_alibi_topk_kernel(tc, qT, k_words, k_scales, ps, sl, pq, offs, o
         raw = [sb.tile([P, 4, NQ], F32, name="raw%d" % g, tag="raw%d" % g, align_bytes=64) for g in range(PASSES)]
 
         nc.gpsimd.memset(zero[:], 0.0)
+        nc.gpsimd.memset(row_consts[96:P, :], 0.0)
         nc.vector.memset(pos_win[0:LAST, :], 0.0)
-        nc.vector.memset(scale_win[0:96, :].bitcast(I32), 0)
+        nc.vector.memset(scale_win[32:64, :].bitcast(I32), 0)
+        nc.vector.memset(scale_win[64:P, :].bitcast(I32), 0)
         make_identity(nc, ident[:])
         nc.gpsimd.memset(key_planes[:].rearrange("p g n -> p (g n)").bitcast(I32), 0)
 
@@ -52,12 +55,13 @@ def tile_attend_alibi_topk_kernel(tc, qT, k_words, k_scales, ps, sl, pq, offs, o
         words = k_words[0].rearrange("p t b -> p (t b)").bitcast(I32)
 
         nc.scalar.dma_start(row_consts[ROWS:ROWS + TILES, :], pq[0].rearrange("(m p) o -> m (p o)", p=P))
-        nc.scalar.dma_start(row_consts[ROWS + TILES:P, :], sl[0].rearrange("(m p) o -> m (p o)", p=P))
+        nc.scalar.dma_start(row_consts[ROWS + TILES:96, :], sl[0].rearrange("(m p) o -> m (p o)", p=P))
         nc.scalar.copy(row_consts[0:ROWS, :], zero[0:ROWS, :].to_broadcast([ROWS, P]))
+        nc.sync.dma_start(word_win[:, 0:AHEAD].bitcast(I32), words[:, 0:AHEAD])
         nc.sync.dma_start(offsets[:], offs)
-        nc.sync.dma_start(scale_win[96:P, :].bitcast(I32), scale_rows)
+        nc.sync.dma_start(scale_win[0:32, :].bitcast(I32), scale_rows)
         nc.sync.dma_start(pos_win[LAST:P, :], ps[0:1, :])
-        nc.sync.dma_start(word_win[:].bitcast(I32), words)
+        nc.sync.dma_start(word_win[:, AHEAD:T].bitcast(I32), words[:, AHEAD:T])
         nc.sync.dma_start(raw[0][:], q_rows[0])
         nc.sync.dma_start(raw[1][:], q_rows[1])
 
@@ -69,31 +73,39 @@ def tile_attend_alibi_topk_kernel(tc, qT, k_words, k_scales, ps, sl, pq, offs, o
         for h in range(2):
             nc.scalar.activation(pos_g[h], listed(pos_win, h * HALF, HALF), ACT.Copy)
             for c in range(2):
-                nc.tensor.transpose(turned[:, 2 * h + c, :], pos_g[h][:, c * P:(c + 1) * P], ident[:])
+                block = 2 * h + c
+                if block == 0:
+                    nc.tensor.matmul(
+                        turned[:, block, :], row_consts[:], ident[:], start=True, stop=False, is_transpose=True
+                    )
+                nc.tensor.matmul(
+                    turned[:, block, :], pos_g[h][:, c * P:(c + 1) * P], ident[:],
+                    start=block > 0, stop=True, is_transpose=True,
+                )
 
         scale_g = sb.tile([P, N], U8, name="scale_g", align_bytes=64)
         nc.vector.tensor_copy(scale_g[:], listed(scale_win, 0, N))
         for q in range(4):
             nc.sync.dma_start(
-                key_planes[32 * q:32 * q + 4].bitcast(I32), scale_g[96 + 8 * q:96 + 8 * q + 8, :].bitcast(I32)
+                key_planes[32 * q:32 * q + 4].bitcast(I32), scale_g[8 * q:8 * q + 8, :].bitcast(I32)
             )
 
-        pos_col = sb.tile([P, 4], F32, name="pos_col")
-        nc.scalar.copy(pos_col[:], turned[:, :, LAST])
-        consts_t = psum.tile([P, P], F32, name="consts_t", tag="turned")
-        nc.tensor.transpose(consts_t[:], row_consts[:], ident[:])
-        consts = sb.tile([P, 2 * TILES], F32, name="consts")
-        nc.scalar.copy(consts[:], consts_t[:, ROWS:P])
+        columns = sb.tile([P, 4, 2, 4], F32, name="columns")
+        nc.scalar.copy(columns[:], turned[:, :, 64:P].rearrange("p c (a b) -> p c a b", a=2)[:, :, :, 28:32])
+        consts = columns[:, 0, 0]
         spread = psum.tile([P, N], F32, name="spread")
         for c in range(4):
-            nc.tensor.transpose(spread[:, c * P:(c + 1) * P], pos_col[:, c:c + 1].to_broadcast([P, P]), ident[:])
+            nc.tensor.transpose(spread[:, c * P:(c + 1) * P], columns[:, c, 1, 3:4].to_broadcast([P, P]), ident[:])
 
         word_g = sb.tile([P, N], U32, name="word_g", align_bytes=64)
         pairs = word_g[:].bitcast(U16).rearrange("p (n g) -> p g n", g=PASSES)
         for h in range(2):
             nc.vector.tensor_copy(word_g[:, h * HALF:(h + 1) * HALF], listed(word_win, h * HALF, HALF))
 
-        keys = {}
+        keys = sb.tile([P, PASSES, N], U16, name="keys", align_bytes=64)
+        for g in range(PASSES):
+            nc.vector.tensor_copy(keys[:, g], pairs[:, g])
+
         codes = {}
         planes = {}
         grouped = {}
@@ -113,25 +125,17 @@ def tile_attend_alibi_topk_kernel(tc, qT, k_words, k_scales, ps, sl, pq, offs, o
                 in_=grouped[g, m].rearrange("p c t -> p (c t)"),
             )
 
-        def part(g, h, tag):
-            keys[g, h] = sb.tile([P, HALF], U16, name="keys%d%d" % (g, h), tag=tag, align_bytes=64)
-            nc.vector.tensor_copy(keys[g, h][:], pairs[:, g, h * HALF:(h + 1) * HALF])
-
         grouped0 = sb.tile([P, TILES, P, 4], BF16, name="grouped0", tag="early", align_bytes=64)
         for m in range(TILES):
             grouped[0, m] = grouped0[:, m]
             grouped[1, m] = sb.tile([P, P, 4], BF16, name="grouped1%d" % m, tag="grouped1%d" % m, align_bytes=64)[:]
 
-        part(0, 0, "keys00")
-        part(0, 1, "keys01")
-        part(1, 0, "keys10")
         cast(nc.scalar.copy, 0, 0, 0, P)
         quantise(0, 0)
         cast(nc.scalar.copy, 0, 1, 0, P)
         quantise(0, 1)
         cast(nc.scalar.copy, 1, 0, SHARE, P)
         cast(nc.vector.tensor_copy, 1, 0, 0, SHARE)
-        part(1, 1, "early")
         quantise(1, 0)
         cast(nc.scalar.copy, 1, 1, 0, P)
         quantise(1, 1)
@@ -142,9 +146,9 @@ def tile_attend_alibi_topk_kernel(tc, qT, k_words, k_scales, ps, sl, pq, offs, o
             for slots in (slice(0, HALF), slice(HALF, N)):
                 nc.scalar.activation(dist[m][:, slots], spread[:, slots], ACT.Abs, bias=consts[:, m:m + 1], scale=-1.0)
 
-        pieces = [(0, 0, P), (0, P, P), (0, HALF, HALF), (1, 0, HALF), (1, HALF, P), (1, HALF + P, P)]
+        pieces = [(0, 0, HALF), (0, HALF, HALF), (1, 0, HALF), (1, HALF, P), (1, HALF + P, P)]
         banks = [
-            psum.tile([P, width], F32, name="bank%d" % i, tag="turned" if i == len(pieces) - 1 else "bank%d" % i)
+            psum.tile([P, width], F32, name="bank%d" % i, tag="bank%d" % (i % 4))
             for i, (m, start, width) in enumerate(pieces)
         ]
 
@@ -154,7 +158,7 @@ def tile_attend_alibi_topk_kernel(tc, qT, k_words, k_scales, ps, sl, pq, offs, o
                 out=banks[i][:],
                 lhsT=codes[g, m][:].bitcast(FP8X4),
                 lhsT_scale=planes[g, m][:],
-                rhs=keys[g, start // HALF][:, start % HALF:start % HALF + width].bitcast(FP4X4),
+                rhs=keys[:, g, start:start + width].bitcast(FP4X4),
                 rhs_scale=key_planes[:, g, start:start + width],
                 start=(g == 0),
                 stop=(g == PASSES - 1),
@@ -175,13 +179,13 @@ def tile_attend_alibi_topk_kernel(tc, qT, k_words, k_scales, ps, sl, pq, offs, o
             slots = slice(pieces[first][1], pieces[last][1] + pieces[last][2])
             nc.sync.dma_start(out[0, m * P:(m + 1) * P, slots], results[:, m, slots])
 
-        for i in range(3):
+        first_of_store = {1: 0, 2: 2, 4: 3}
+        for i in range(2):
             multiply(i, 0)
         for i in range(len(pieces)):
-            if i >= 3:
+            if i >= 2:
                 multiply(i, 0)
             multiply(i, 1)
             finish(i)
-            if i < 4:
-                store(i, i)
-        store(4, 5)
+            if i in first_of_store:
+                store(first_of_store[i], i)

@@ -103,8 +103,12 @@ def tile_attend_alibi_topk_kernel(tc, qT, k_words, k_scales, ps, sl, pq, offs, o
             nc.vector.tensor_copy(word_g[:, h * HALF:(h + 1) * HALF], listed(word_win, h * HALF, HALF))
 
         keys = sb.tile([P, PASSES, N], U16, name="keys", align_bytes=64)
-        for g in range(PASSES):
-            nc.vector.tensor_copy(keys[:, g], pairs[:, g])
+        for h in range(2):
+            slots = slice(h * HALF, (h + 1) * HALF)
+            nc.vector.tensor_copy(
+                keys[:, :, slots].rearrange("p g (c i) -> p c g i", i=8),
+                pairs[:, :, slots].rearrange("p g (c i) -> p c g i", i=8),
+            )
 
         codes = {}
         planes = {}

from contextlib import ExitStack

import concourse.mybir as mybir
from concourse.masks import make_identity

F32 = mybir.dt.float32
BF16 = mybir.dt.bfloat16
I32 = mybir.dt.int32
U32 = mybir.dt.uint32
U16 = mybir.dt.uint16
U8 = mybir.dt.uint8
FP8X4 = mybir.dt.float8_e4m3fn_x4
FP4X4 = mybir.dt.float4_e2m1fn_x4
ALU = mybir.AluOpType
ACT = mybir.ActivationFunctionType

P = 128
N, T, D, NQ = 512, 2048, 1024, 256
PASSES = D // 512
TILES = NQ // P
FLOPS = 2 * NQ * N * D


def tile_attend_alibi_topk_kernel(tc, qT, k_words, k_scales, ps, sl, pq, offs, out):
    nc = tc.nc
    with ExitStack() as ctx:
        sb = ctx.enter_context(tc.tile_pool(name="sb", bufs=1))
        psum = ctx.enter_context(tc.psum_pool(name="psum", bufs=1))
        LAST = P - 1
        ROWS = 96 - 2 * TILES
        HALF = N // 2
        AHEAD = T // 8
        SHARE = 96

        offsets = sb.tile([P, N // 16], U16, name="offsets")
        pos_win = sb.tile([P, T], F32, name="pos_win", align_bytes=64)
        scale_win = sb.tile([P, T], U8, name="scale_win", align_bytes=64)
        word_win = sb.tile([P, T], U32, name="word_win", align_bytes=64)
        key_planes = sb.tile([P, PASSES, N], U8, name="key_planes", align_bytes=64)
        ident = sb.tile([P, P], F32, name="ident", align_bytes=64)
        zero = sb.tile([P, 1], F32, name="zero")
        row_consts = sb.tile([P, P], F32, name="row_consts", align_bytes=64)
        raw = [sb.tile([P, 4, NQ], F32, name="raw%d" % g, tag="raw%d" % g, align_bytes=64) for g in range(PASSES)]

        nc.gpsimd.memset(zero[:], 0.0)
        nc.gpsimd.memset(row_consts[96:P, :], 0.0)
        nc.vector.memset(pos_win[0:LAST, :], 0.0)
        nc.vector.memset(scale_win[32:64, :].bitcast(I32), 0)
        nc.vector.memset(scale_win[64:P, :].bitcast(I32), 0)
        make_identity(nc, ident[:])
        nc.gpsimd.memset(key_planes[:].rearrange("p g n -> p (g n)").bitcast(I32), 0)

        q_rows = qT[0].rearrange("(g p t) c -> g p t c", g=PASSES, t=4)
        scale_rows = k_scales.bitcast(I32).rearrange("o f n -> f o n")
        words = k_words[0].rearrange("p t b -> p (t b)").bitcast(I32)

        nc.scalar.dma_start(row_consts[ROWS:ROWS + TILES, :], pq[0].rearrange("(m p) o -> m (p o)", p=P))
        nc.scalar.dma_start(row_consts[ROWS + TILES:96, :], sl[0].rearrange("(m p) o -> m (p o)", p=P))
        nc.scalar.copy(row_consts[0:ROWS, :], zero[0:ROWS, :].to_broadcast([ROWS, P]))
        nc.sync.dma_start(word_win[:, 0:AHEAD].bitcast(I32), words[:, 0:AHEAD])
        nc.sync.dma_start(offsets[:], offs)
        nc.sync.dma_start(scale_win[0:32, :].bitcast(I32), scale_rows)
        nc.sync.dma_start(pos_win[LAST:P, :], ps[0:1, :])
        nc.sync.dma_start(word_win[:, AHEAD:T].bitcast(I32), words[:, AHEAD:T])
        nc.sync.dma_start(raw[0][:], q_rows[0])
        nc.sync.dma_start(raw[1][:], q_rows[1])

        def listed(window, first, count):
            return window[:].indirect(offsets[:, first // 16:(first + count) // 16])

        turned = psum.tile([P, 4, P], F32, name="turned", tag="turned")
        pos_g = [sb.tile([P, HALF], F32, name="pos_g0", align_bytes=64)[:], sb.tile([P, HALF], F32, name="pos_g1", tag="early", align_bytes=64)[:]]
        for h in range(2):
            nc.scalar.activation(pos_g[h], listed(pos_win, h * HALF, HALF), ACT.Copy)
            for c in range(2):
                block = 2 * h + c
                if block == 0:
                    nc.tensor.matmul(
                        turned[:, block, :], row_consts[:], ident[:], start=True, stop=False, is_transpose=True
                    )
                nc.tensor.matmul(
                    turned[:, block, :], pos_g[h][:, c * P:(c + 1) * P], ident[:],
                    start=block > 0, stop=True, is_transpose=True,
                )

        scale_g = sb.tile([P, N], U8, name="scale_g", align_bytes=64)
        nc.vector.tensor_copy(scale_g[:], listed(scale_win, 0, N))
        for q in range(4):
            nc.sync.dma_start(
                key_planes[32 * q:32 * q + 4].bitcast(I32), scale_g[8 * q:8 * q + 8, :].bitcast(I32)
            )

        columns = sb.tile([P, 4, 2, 4], F32, name="columns")
        nc.scalar.copy(columns[:], turned[:, :, 64:P].rearrange("p c (a b) -> p c a b", a=2)[:, :, :, 28:32])
        consts = columns[:, 0, 0]
        spread = psum.tile([P, N], F32, name="spread")
        for c in range(4):
            nc.tensor.transpose(spread[:, c * P:(c + 1) * P], columns[:, c, 1, 3:4].to_broadcast([P, P]), ident[:])

        word_g = sb.tile([P, N], U32, name="word_g", align_bytes=64)
        pairs = word_g[:].bitcast(U16).rearrange("p (n g) -> p g n", g=PASSES)
        for h in range(2):
            nc.vector.tensor_copy(word_g[:, h * HALF:(h + 1) * HALF], listed(word_win, h * HALF, HALF))

        keys = sb.tile([P, PASSES, N], U16, name="keys", align_bytes=64)
        for h in range(2):
            slots = slice(h * HALF, (h + 1) * HALF)
            nc.vector.tensor_copy(
                keys[:, :, slots].rearrange("p g (c i) -> p c g i", i=8),
                pairs[:, :, slots].rearrange("p g (c i) -> p c g i", i=8),
            )

        codes = {}
        planes = {}
        grouped = {}

        def cast(copy, g, m, first, end):
            copy(
                grouped[g, m][:, first:end, :].rearrange("p (c i) t -> p c t i", i=4),
                raw[g][:, :, m * P + first:m * P + end].rearrange("p t (c i) -> p c t i", i=4),
            )

        def quantise(g, m):
            codes[g, m] = sb.tile([P, P], U32, name="codes%d%d" % (g, m), align_bytes=64)
            planes[g, m] = sb.tile([P, P], U8, name="plane%d%d" % (g, m), align_bytes=64)
            nc.vector.quantize_mx(
                out=codes[g, m][:].bitcast(FP8X4),
                scales=planes[g, m][:],
                in_=grouped[g, m].rearrange("p c t -> p (c t)"),
            )

        grouped0 = sb.tile([P, TILES, P, 4], BF16, name="grouped0", tag="early", align_bytes=64)
        for m in range(TILES):
            grouped[0, m] = grouped0[:, m]
            grouped[1, m] = sb.tile([P, P, 4], BF16, name="grouped1%d" % m, tag="grouped1%d" % m, align_bytes=64)[:]

        cast(nc.scalar.copy, 0, 0, 0, P)
        quantise(0, 0)
        cast(nc.scalar.copy, 0, 1, 0, P)
        quantise(0, 1)
        cast(nc.scalar.copy, 1, 0, SHARE, P)
        cast(nc.vector.tensor_copy, 1, 0, 0, SHARE)
        quantise(1, 0)
        cast(nc.scalar.copy, 1, 1, 0, P)
        quantise(1, 1)

        dist_all = sb.tile([P, TILES, N], F32, name="dist_all", tag="raw1", align_bytes=64)
        dist = [dist_all[:, m] for m in range(TILES)]
        for m in range(TILES):
            for slots in (slice(0, HALF), slice(HALF, N)):
                nc.scalar.activation(dist[m][:, slots], spread[:, slots], ACT.Abs, bias=consts[:, m:m + 1], scale=-1.0)

        pieces = [(0, 0, HALF), (0, HALF, HALF), (1, 0, HALF), (1, HALF, P), (1, HALF + P, P)]
        banks = [
            psum.tile([P, width], F32, name="bank%d" % i, tag="bank%d" % (i % 4))
            for i, (m, start, width) in enumerate(pieces)
        ]

        def multiply(i, g):
            m, start, width = pieces[i]
            nc.tensor.matmul_mx(
                out=banks[i][:],
                lhsT=codes[g, m][:].bitcast(FP8X4),
                lhsT_scale=planes[g, m][:],
                rhs=keys[:, g, start:start + width].bitcast(FP4X4),
                rhs_scale=key_planes[:, g, start:start + width],
                start=(g == 0),
                stop=(g == PASSES - 1),
            )

        results = sb.tile([P, TILES, N], F32, name="results", align_bytes=64)

        def finish(i):
            m, start, width = pieces[i]
            slots = slice(start, start + width)
            nc.vector.scalar_tensor_tensor(
                results[:, m, slots], dist[m][:, slots], consts[:, TILES + m:TILES + m + 1], banks[i][:],
                ALU.mult, ALU.subtract, reverse1=True,
            )

        def store(first, last):
            m = pieces[first][0]
            slots = slice(pieces[first][1], pieces[last][1] + pieces[last][2])
            nc.sync.dma_start(out[0, m * P:(m + 1) * P, slots], results[:, m, slots])

        first_of_store = {1: 0, 2: 2, 4: 3}
        for i in range(2):
            multiply(i, 0)
        for i in range(len(pieces)):
            if i >= 2:
                multiply(i, 0)
            multiply(i, 1)
            finish(i)
            if i in first_of_store:
                store(first_of_store[i], i)
